import numpy as np, ml_dtypes
CORES = [66,74,82,90,194,202,210,218]
N = 8
import mx_ref
BF = ml_dtypes.bfloat16
def entries(a):
    return np.ascontiguousarray(a.T).reshape(-1)
def table(e):
    return np.ascontiguousarray(np.reshape(e, (-1, 16)).T).astype(np.int32)
def cols(t, e):
    v = np.concatenate([t.reshape(128, -1, 4), np.zeros((128, 1, 4), BF)], axis=1)
    return np.ascontiguousarray(v[:, e]).reshape(128, -1)
def f(rng, *shape):
    return mx_ref.flush((rng.standard_normal(shape, dtype=np.float32) * np.exp2(rng.integers(-2, 3, shape[:-1] + (1,)))).astype(BF))
def wide(rng, *shape, cols=0):
    v = rng.standard_normal(shape, dtype=np.float32) * np.exp2(rng.integers(-12, 13, shape)).astype(np.float32)
    if cols: v *= np.repeat(np.exp2(rng.integers(-cols, cols + 1, shape[:-2] + (1, shape[-1] // 4))) * (rng.random(shape[:-2] + (1, shape[-1] // 4)) > 0.0625), 4, axis=-1).astype(np.float32)
    return mx_ref.flush(v.astype(BF))
T, B, NB, SUM = 512, 256, 3, 768
SIDE = np.array([0 if c < 128 else 1 for c in CORES])
CAP = np.where(SIDE[:, None] == SIDE[None, :], 96, 96)
ST = np.cumsum(CAP, axis=1) - CAP
def lists(rng, alone=False, same=False, full=False, last=False):
    it, it2, ob, bag = np.full((N, SUM), -1), np.full((N, SUM), -1), np.full((N, SUM), -1), np.full((N, SUM), -1)
    one = rng.integers(0, T, N)
    none = rng.permutation(N) if alone else np.full(N, -1)
    for r in range(N):
        has = np.zeros((N, B), bool)
        free = np.where(np.arange(N) == none[r], 0, CAP[:, r])
        if full: has[:, rng.integers(0, B)] = True
        g = np.flatnonzero(~has.any(axis=0))
        has[rng.permutation(np.repeat(np.arange(N), free - has.sum(axis=1)))[:len(g)], g] = True
        for s in range(N):
            n = CAP[s, r]; h = has[s].sum()
            k = n if full else rng.integers(h, free[s] + 1)
            has[s, rng.permutation(np.flatnonzero(~has[s]))[:k - h]] = True
            j = np.flatnonzero(has[s]); c = rng.permutation(n)[:k]
            if last: j, c = j[::-1], np.sort(c)
            else: j = rng.permutation(j)
            u = np.full(k, one[s]) if same else rng.integers(0, T, k)
            v = (u + rng.integers(1, T, k)) % T if same else rng.integers(0, T, k)
            v = np.where(rng.random(k) < (1.0 if alone else 0.25), -1, v)
            it[s, ST[s, r] + c] = u; it2[s, ST[s, r] + c] = v; ob[s, ST[s, r] + c] = j; bag[r, ST[r, s] + c] = j
    return {"it": np.stack([table(e) for e in it]), "it2": np.stack([table(e) for e in it2]), "ob": np.stack([table(e) for e in ob]), "bag": np.stack([table(e) for e in bag])}
def setup_inputs(rng):
    return {"ex": f(rng, N, 128, 4 * T), "w": f(rng, N, 128, 512 * NB), **lists(rng)}
def setup_inputs_alone(rng):
    return {**setup_inputs(rng), **lists(rng, alone=True)}
def setup_inputs_full(rng):
    return {**setup_inputs(rng), **lists(rng, full=True)}
def setup_inputs_last(rng):
    return {**setup_inputs(rng), **lists(rng, last=True)}
def setup_inputs_same(rng):
    return {**setup_inputs(rng), **lists(rng, same=True)}
def setup_inputs_spread(rng):
    d = setup_inputs(rng); d["ex"] = wide(rng, N, 128, 4 * T, cols=6); return d
def check_inputs(d):
    b = []
    it, it2, ob, bag = [np.stack([entries(d[k][r]) for r in range(N)]) for k in ("it", "it2", "ob", "bag")]
    if it.min() < -1 or it.max() >= T: b.append("it")
    if it2.min() < -1 or it2.max() >= T: b.append("it2")
    if (it2[it < 0] != -1).any(): b.append("a second item in an empty slot")
    if ob.min() < -1 or ob.max() >= B: b.append("ob")
    if bag.min() < -1 or bag.max() >= B: b.append("bag")
    for r in range(N):
        for s in range(N):
            n = CAP[s, r]; u = it[s, ST[s, r]:ST[s, r] + n]; j = bag[r, ST[r, s]:ST[r, s] + n]
            if ((u < 0) != (j < 0)).any(): b.append("bag and it differ in their empty slots")
            if (ob[s, ST[s, r]:ST[s, r] + n] != j).any(): b.append("ob and bag differ")
            j = j[j >= 0]
            if len(set(j.tolist())) != len(j): b.append("a bag named twice")
        if not set(range(B)) <= set(bag[r].tolist()): b.append("a bag without parts")
    return b
def reference(ex, w, it, it2, ob, bag):
    y = np.zeros((N, 128, B * NB), np.float32)
    for r in range(N):
        W = [mx_ref.quantize(w[r][:, 512 * o:512 * o + 512]) for o in range(NB)]
        for s in range(N):
            n = CAP[s, r]
            u, v = entries(it[s])[ST[s, r]:ST[s, r] + n], entries(it2[s])[ST[s, r]:ST[s, r] + n]
            part = (cols(ex[s], u).astype(np.float32) + cols(ex[s], v).astype(np.float32)).astype(BF)
            P = mx_ref.quantize(part)
            j = entries(bag[r])[ST[r, s]:ST[r, s] + n]; used = j >= 0
            for o in range(NB): y[r][:, B * o + j[used]] += mx_ref.matmul(W[o], P)[:, used]
    return {"y": y}

@@ -1,0 +1,313 @@
+from concourse.bass import DstId, RemoteDMATransfer
+from concourse.mybir import dt, AluOpType, ActivationFunctionType
+
+N, CAP, BAGS, NB, ITEMS = 8, 96, 256, 3, 512
+PAIR = 2 * CAP
+LC = CAP // 16
+LIST = N * LC
+ZERO = 16
+WIN = ZERO + 4 * ITEMS
+INV = 464
+SL = 8
+ZW = SL + N * CAP
+HB = CAP // 32
+NC = BAGS // 32
+RAW = N * HB + NC
+HOME = N * LC
+F32, BF, I32, U16 = "float32", "bfloat16", "int32", "uint16"
+SCRATCH = {
+    "exw": ("sbuf", [128, WIN], BF),
+    "wt": ("sbuf", [128, 512 * NB], BF),
+    "wq": ("sbuf", [128, 128 * NB], "float8_e4m3fn_x4"),
+    "wsc": ("sbuf", [128, 128 * NB], "uint8"),
+    "lraw": ("sbuf", [128, 2 * LIST], I32),
+    "hu": ("sbuf", [128, 4 * N * CAP], BF),
+    "h": ("sbuf", [128, 4 * N * CAP], BF),
+    "q": ("sbuf", [128, N * CAP], "float8_e4m3fn_x4"),
+    "qsc": ("sbuf", [128, N * CAP], "uint8"),
+    "lq": ("sbuf", [128, N * CAP], "float8_e4m3fn_x4"),
+    "lsc": ("sbuf", [128, N * CAP], "uint8"),
+    "bagg": ("sbuf", [128, LC], I32),
+    "neg": ("sbuf", [128, LC], I32),
+    "dumpo": ("sbuf", [128, LC], I32),
+    "dmp": ("sbuf", [128, LC], I32),
+    "bo": ("sbuf", [128, LC], I32),
+    "boff": ("sbuf", [128, LC], U16),
+    "ip": ("sbuf", [128, 1], I32),
+    "ip2": ("sbuf", [128, 1], I32),
+    "ipf": ("sbuf", [128, 1], F32),
+    "io1": ("sbuf", [128, CAP], F32),
+    "vals": ("sbuf", [128, CAP], F32),
+    "inv": ("sbuf", [128, INV], F32),
+    "invt": ("sbuf", [128, BAGS], F32),
+    "pm": ("sbuf", [128, NC], F32),
+    "prt": ("sbuf", [128, BAGS], F32),
+    "prw": ("sbuf", [128, INV], F32),
+    "pv": ("sbuf", [128, CAP], F32),
+    "pvt": ("sbuf", [128, CAP], F32),
+    "cc": ("sbuf", [128, 16], F32),
+    "raw": ("sbuf", [32, 2 * RAW], F32),
+    "offb": ("sbuf", [128, 2 * RAW], U16),
+    "acc": ("sbuf", [128, NB * BAGS], F32),
+    "ps": ("psum", [128, 4096], F32),
+}
+for _t in range(4):
+    SCRATCH["off%d" % _t] = ("sbuf", [128, 2 * LIST], U16)
+for _k in range(NB):
+    SCRATCH["z%d" % _k] = ("sbuf", [128, ZW], F32)
+SEMAPHORES = ["ldl", "ldx", "ldb", "ldw", "ldr", "vs", "ss", "ps", "gs", "loc", "st", "a0", "a1", "a2", "a3"]
+
+
+def rank_program(g, core, T, topo):
+    r = T.rank_of(core)
+    if r is None:
+        return
+    Alu, Copy = AluOpType, ActivationFunctionType.Copy
+    V = g.vector
+    order = sorted(range(1, N // 2), key=lambda x: (topo.host(T.cores[2 * x]) == topo.host(T.cores[0]), -x)) + [0]
+    NCH = len(order)
+    peers = [[2 * (r // 2 ^ x) + m for m in range(2)] for x in order]
+    mem, mate = r % 2, r ^ 1
+    owners = peers[0] + peers[1] + [r] + peers[2] + [mate]
+
+    cnt = {"vs": 0, "ss": 0, "ps": 0, "gs": 0}
+    seen = {}
+    queues = {"v": g.vector, "s": g.scalar, "t": g.tensor, "y": g.sync, "g": g}
+
+    def need(qn, sem, val):
+        if val > seen.get((qn, sem), 0):
+            queues[qn].wait_ge(T.sem[sem], val)
+            seen[(qn, sem)] = val
+
+    def did(sem, ins):
+        ins.then_inc(T.sem[sem], 1)
+        cnt[sem] += 1
+        return cnt[sem]
+
+    for grp in range(2):
+        g.sync.dma_start(T.lraw[16 * grp:16 * grp + 16, 0:LIST], T["it"][:, :]).then_inc(T.sem.ldl, 16)
+        g.scalar.dma_start(T.lraw[16 * grp:16 * grp + 16, LIST:2 * LIST], T["it2"][:, :]).then_inc(T.sem.ldl, 16)
+    for i, s in enumerate(owners):
+        q = g.scalar if i % 2 else g.sync
+        q.dma_start(T.bagg[16 * i:16 * i + 16, :], T.bag[:, LC * s:LC * s + LC]).then_inc(T.sem.ldb, 16)
+    g.sync.dma_start(T.exw[:, ZERO:WIN], T.ex[:, :]).then_inc(T.sem.ldx, 16)
+    g.sync.dma_start(T.wt[:, :], T.w[:, :]).then_inc(T.sem.ldw, 16)
+
+    def zeros(ap, n):
+        return did("gs", g.iota(ap, [[0, n]], 0, 0, allow_small_or_imprecise_dtypes=True))
+    g_ip = did("gs", g.iota(T.ip[:, :], [[1, 1]], 0, 1))
+    g_io = did("gs", g.iota(T.io1[:, :], [[1, CAP]], 0, 0, allow_small_or_imprecise_dtypes=True))
+    g_du = did("gs", g.iota(T.dumpo[:, :], [[16, LC]], BAGS + 1, 1))
+    g_pt = zeros(T.prt[:, :], BAGS)
+    g_pw = zeros(T.prw[:, BAGS:INV], INV - BAGS)
+    for o in range(NB):
+        g_z = zeros(T["z%d" % o][:, 0:SL], SL)
+    did("vs", V.memset(T.exw[:, 0:ZERO], 0.0))
+    did("vs", V.memset(T.inv[:, :], 0.0))
+    need("v", "gs", g_ip)
+    k = did("vs", V.tensor_scalar(T.ip2[:, :], T.ip[:, :], 4, None, Alu.arith_shift_right))
+    need("v", "vs", k)
+    k = did("vs", V.tensor_scalar(T.ipf[:, :], T.ip2[:, :], float(CAP), float(SL), Alu.mult, Alu.add))
+    need("v", "gs", g_io)
+    need("v", "vs", k)
+    did("vs", V.tensor_scalar(T.vals[:, :], T.io1[:, :], T.ipf[:, 0:1], None, Alu.add))
+
+    last = [0]
+    steps = []
+
+    def step(f, *waits):
+        def run():
+            for sem, val in waits:
+                need("v", sem, val)
+            need("v", "vs", last[0])
+            last[0] = did("vs", f())
+        steps.append(run)
+
+    def run_steps(n):
+        for f in steps[:n]:
+            f()
+        del steps[:n]
+
+    step(lambda: V.tensor_scalar(T.neg[:, :], T.bagg[:, :], 0, None, Alu.is_lt), ("ldb", 16 * N))
+    step(lambda: V.tensor_tensor(T.dmp[:, :], T.neg[:, :], T.dumpo[:, :], Alu.mult), ("gs", g_du))
+    step(lambda: V.tensor_tensor(T.bo[:, :], T.bagg[:, :], T.dmp[:, :], Alu.add))
+    step(lambda: V.tensor_copy(T.boff[:, :], T.bo[:, :]))
+    step(lambda: V.tensor_copy(T.inv[:, 0:INV].indirect(T.boff[:, 0:LC]), T.vals[:, :]))
+    step(lambda: V.transpose(T.invt[:, :], T.inv[:, 0:BAGS]))
+    step(lambda: V.tensor_tensor(T.pm[:, :], T.invt[:, 0:BAGS:32], T.invt[:, 16:BAGS:32], Alu.max))
+    for a in range(1, 4):
+        p, n = 32 * a - 32, 32 * a
+        step(lambda p=p, n=n: V.tensor_copy(T.prt[n:n + 32, 0:BAGS:32], T.pm[p:p + 32, :]), ("gs", g_pt))
+        to = T.pm[n:n + 32, :] if a < 3 else T.cc[n:n + 32, 2 * HB:2 * HB + NC]
+        step(lambda n=n, to=to: V.tensor_tensor(to, T.prt[n:n + 32, 0:BAGS:32], T.pm[n:n + 32, :], Alu.max))
+    step(lambda: V.tensor_tensor(T.prt[:, 16:BAGS:32], T.prt[:, 0:BAGS:32], T.invt[:, 0:BAGS:32], Alu.max))
+    step(lambda: V.transpose(T.prw[:, 0:BAGS], T.prt[:, :]))
+    step(lambda: V.tensor_copy(T.pv[:, :], T.prw[:, 0:INV].indirect(T.boff[:, 0:LC])), ("gs", g_pw))
+    step(lambda: V.transpose(T.pvt[:, :], T.pv[:, :]))
+
+    def extract():
+        need("v", "vs", last[0])
+        for hh in range(2):
+            last[0] = did("vs", V.tensor_copy(T.cc[:, HB * hh:HB * hh + HB], T.pvt[:, 16 * hh:CAP:32]))
+        need("y", "vs", last[0])
+        for a in range(4):
+            n = 2 * HB + (NC if a == 3 else 0)
+            for hh in range(2):
+                for grp in range(2):
+                    b = RAW * hh + 2 * HB * a
+                    g.sync.dma_start(T.raw[16 * grp:16 * grp + 16, b:b + n],
+                                     T.cc[32 * a + 16 * hh:32 * a + 16 * hh + 16, 0:n]).then_inc(T.sem.ldr, 16)
+
+    def spread():
+        need("v", "ldr", 16 * 16)
+        for hh in range(2):
+            last[0] = did("vs", V.tensor_copy(T.offb[0:32, hh:2 * RAW:2], T.raw[:, RAW * hh:RAW * hh + RAW]))
+
+    def spread_on():
+        need("v", "vs", last[0])
+        for qd in range(1, 4):
+            last[0] = did("vs", V.tensor_copy(T.offb[32 * qd:32 * qd + 32, :], T.offb[0:32, :]))
+
+    need("v", "ldl", 64)
+    for qd in range(1, 4):
+        k = did("vs", V.tensor_copy(T.lraw[32 * qd:32 * qd + 32, :], T.lraw[0:32, :]))
+    run_steps(1)
+    need("v", "vs", k)
+    v_off = []
+    for t in range(4):
+        v_off.append(did("vs", V.tensor_scalar(T["off%d" % t][:, :], T.lraw[:, :], 4.0, float(ZERO + t), Alu.mult, Alu.add)))
+        run_steps(1)
+    run_steps(4)
+
+    s_u = {}
+    need("s", "ldx", 16)
+    for c in range(NCH):
+        l = LC * peers[c][0]
+        for t in range(4):
+            need("s", "vs", v_off[t])
+            b = (4 * c + t) * PAIR
+            s_u[c, t] = did("ss", g.scalar.activation(T.hu[:, b:b + PAIR], T.exw[:, 0:WIN].indirect(T["off%d" % t][:, l:l + 2 * LC]), Copy))
+    v_h = [0] * NCH
+    v_q = [0] * NCH
+
+    def part(c, t):
+        need("v", "ldx", 16)
+        need("v", "vs", v_off[t])
+        need("v", "ss", s_u[c, t])
+        b = (4 * c + t) * PAIR
+        l = LIST + LC * peers[c][0]
+        v_h[c] = did("vs", V.tensor_tensor(T.h[:, 4 * c * PAIR + t:4 * (c + 1) * PAIR:4],
+                                           T.exw[:, 0:WIN].indirect(T["off%d" % t][:, l:l + 2 * LC]), T.hu[:, b:b + PAIR], Alu.add))
+
+    def quant(c):
+        need("v", "vs", v_h[c])
+        a, b = c * PAIR, (c + 1) * PAIR
+        v_q[c] = did("vs", V.quantize_mx(T.q[:, a:b], T.qsc[:, a:b], T.h[:, 4 * a:4 * b]))
+
+    for t in range(4):
+        part(0, t)
+        run_steps(1)
+    run_steps(1)
+    quant(0)
+    for t in range(3):
+        part(1, t)
+        run_steps(1)
+    part(1, 3)
+    extract()
+    part(2, 0)
+    quant(1)
+    for t in range(1, 4):
+        part(2, t)
+    part(3, 0)
+    quant(2)
+    need("v", "ldw", 16)
+    v_w = did("vs", V.quantize_mx(T.wq[:, :], T.wsc[:, :], T.wt[:, :]))
+    for t in range(1, 4):
+        part(3, t)
+    spread()
+    quant(3)
+    spread_on()
+
+    loc = 0
+    arr = []
+    for c in range(NCH):
+        dests = [d for d in peers[c] if d != r]
+        need("g", "vs", v_q[c])
+        for kind in range(2):
+            tr, tot = [], 0
+            for i, d in enumerate(dests):
+                dst = T.cores[d]
+                eng = topo.engines(core, dst)
+                n = len(eng) // len(dests)
+                rid, pnc = topo.addr(dst, core)
+                a = c * PAIR + CAP * (d % 2)
+                b = c * PAIR + (CAP * mem if c < NCH - 1 else 0)
+                if kind == 0:
+                    src, out = T.q[:, a:a + CAP].bitcast(dt.uint8), T.lq[:, b:b + CAP].bitcast(dt.uint8)
+                else:
+                    src, out = T.qsc[:, a:a + CAP], T.lsc[:, b:b + CAP]
+                tr.append(RemoteDMATransfer(dst_ids=[DstId(rid=rid, pnc=pnc)], dma_engine_mask=sum(1 << e for e in eng[i * n:(i + 1) * n]),
+                                            remote_sem=T.sem["a%d" % c], src=src, dst=out))
+                tot += n
+            g.remote_dma_fused(tr, local_sem=T.sem.loc)
+            loc += tot
+        arr.append(2 * tot)
+
+    need("t", "vs", v_w)
+    use = 0
+    bank_free = [0] * 8
+    z_in = {}
+    own = (NCH - 1) * PAIR + CAP * mem
+    own_first = min(own, N * CAP - 128)
+    mate_first = (NCH - 1) * PAIR + CAP - 128
+    stages = [(T.lq, T.lsc, 0, 0, PAIR, 0, "a0", arr[0]),
+              (T.lq, T.lsc, PAIR, 0, PAIR, 2, "a1", arr[1]),
+              (T.q, T.qsc, own_first, own - own_first, CAP, 4, "vs", v_q[3]),
+              (T.lq, T.lsc, 2 * PAIR, 0, PAIR, 5, "a2", arr[2]),
+              (T.lq, T.lsc, mate_first, 128 - CAP, CAP, 7, "a3", arr[3])]
+    for src, ssc, first, lo, width, place, sem, val in stages:
+        need("t", sem, val)
+        n = max(128, width)
+        for o in range(NB):
+            bk = use % 8
+            use += 1
+            need("t", "ss", bank_free[bk])
+            p = did("ps", g.tensor.matmul_mx(T.ps[:, 512 * bk:512 * bk + n], T.wq[:, 128 * o:128 * o + 128], T.wsc[:, 128 * o:128 * o + 128],
+                                             src[:, first:first + n], ssc[:, first:first + n], True, True))
+            need("s", "ps", p)
+            b = SL + CAP * place
+            k = did("ss", g.scalar.activation(T["z%d" % o][:, b:b + width], T.ps[:, 512 * bk + lo:512 * bk + lo + width], Copy))
+            bank_free[bk] = k
+            for i in range(width // CAP):
+                z_in[place + i, o] = k
+
+    chain = [0] * NB
+    for i in range(1, N):
+        for o in (0, 2, 1) if i == N - 1 else range(NB):
+            z = T["z%d" % o]
+            b = SL + CAP * i
+            need("v", "gs", g_z)
+            need("v", "vs", max(chain[o], last[0]))
+            need("v", "ss", z_in[i, o])
+            chain[o] = did("vs", V.tensor_tensor(z[:, b:b + CAP], z[:, 0:b].indirect(T.offb[:, LC * i:LC * i + LC]), z[:, b:b + CAP], Alu.add))
+
+    for o in (0, 2, 1):
+        y = T.acc[:, BAGS * o:BAGS * (o + 1)]
+        win = T["z%d" % o][:, 0:ZW].indirect(T.offb[:, HOME:HOME + BAGS // 16])
+        if o == 2:
+            need("v", "vs", chain[o])
+            k = did("vs", V.tensor_copy(y, win))
+            need("y", "vs", k)
+            q = g.sync
+        else:
+            need("s", "gs", g_z)
+            need("s", "vs", chain[o])
+            k = did("ss", g.scalar.activation(y, win, Copy))
+            q = g.scalar if o == 1 else g.sync
+            need("s" if o == 1 else "y", "ss", k)
+        q.dma_start(T.y[:, BAGS * o:BAGS * (o + 1)], y).then_inc(T.sem.st, 16)
+
+    need("g", "loc", loc)
+    for sem in ("gs", "vs", "ss", "ps"):
+        need("g", sem, cnt[sem])
+    need("g", "st", 16 * NB)

@@ -2,7 +2,7 @@ from concourse.bass import DstId, RemoteDMATransfer
 from concourse.mybir import dt, AluOpType, ActivationFunctionType
 
 N, CAP, BAGS, NB, ITEMS = 8, 96, 256, 3, 512
-PAIR = 2 * CAP
+TILE = 128
 LC = CAP // 16
 LIST = N * LC
 ZERO = 16
@@ -10,10 +10,15 @@ WIN = ZERO + 4 * ITEMS
 INV = 464
 SL = 8
 ZW = SL + N * CAP
-HB = CAP // 32
-NC = BAGS // 32
-RAW = N * HB + NC
-HOME = N * LC
+LW = LC + 2
+PV = 32 * LW
+HOME = N * LW
+QW = (N - 2) * CAP + 2 * TILE
+ROWS_AT, T_AT, X_AT, W_AT = 8, 10, 18, 13
+SELF = 1
+PRE = "icccioooiotti"
+TAIL = [(7, 0), (7, 2), (7, 1)]
+PIECES = [("s", 0, 0, BAGS), ("v", 2, 0, BAGS), ("s", 1, 0, BAGS)]
 F32, BF, I32, U16 = "float32", "bfloat16", "int32", "uint16"
 SCRATCH = {
     "exw": ("sbuf", [128, WIN], BF),
@@ -23,31 +28,29 @@ SCRATCH = {
     "lraw": ("sbuf", [128, 2 * LIST], I32),
     "hu": ("sbuf", [128, 4 * N * CAP], BF),
     "h": ("sbuf", [128, 4 * N * CAP], BF),
-    "q": ("sbuf", [128, N * CAP], "float8_e4m3fn_x4"),
-    "qsc": ("sbuf", [128, N * CAP], "uint8"),
-    "lq": ("sbuf", [128, N * CAP], "float8_e4m3fn_x4"),
-    "lsc": ("sbuf", [128, N * CAP], "uint8"),
+    "q": ("sbuf", [128, QW], "float8_e4m3fn_x4"),
+    "qsc": ("sbuf", [128, QW], "uint8"),
+    "lq": ("sbuf", [128, (N - 1) * CAP], "float8_e4m3fn_x4"),
+    "lsc": ("sbuf", [128, (N - 1) * CAP], "uint8"),
     "bagg": ("sbuf", [128, LC], I32),
-    "neg": ("sbuf", [128, LC], I32),
+    "pos": ("sbuf", [128, LC], I32),
     "dumpo": ("sbuf", [128, LC], I32),
-    "dmp": ("sbuf", [128, LC], I32),
-    "bo": ("sbuf", [128, LC], I32),
+    "bo": ("sbuf", [128, LW], I32),
     "boff": ("sbuf", [128, LC], U16),
+    "twice": ("sbuf", [128, 2 * LW], U16),
     "ip": ("sbuf", [128, 1], I32),
     "ip2": ("sbuf", [128, 1], I32),
     "ipf": ("sbuf", [128, 1], F32),
     "io1": ("sbuf", [128, CAP], F32),
     "vals": ("sbuf", [128, CAP], F32),
     "inv": ("sbuf", [128, INV], F32),
-    "invt": ("sbuf", [128, BAGS], F32),
-    "pm": ("sbuf", [128, NC], F32),
-    "prt": ("sbuf", [128, BAGS], F32),
     "prw": ("sbuf", [128, INV], F32),
-    "pv": ("sbuf", [128, CAP], F32),
-    "pvt": ("sbuf", [128, CAP], F32),
-    "cc": ("sbuf", [128, 16], F32),
-    "raw": ("sbuf", [32, 2 * RAW], F32),
-    "offb": ("sbuf", [128, 2 * RAW], U16),
+    "gate": ("sbuf", [128, PV], F32),
+    "pv": ("sbuf", [128, PV], F32),
+    "pvt": ("sbuf", [128, PV], F32),
+    "run": ("sbuf", [128, PV], F32),
+    "raw": ("sbuf", [128, HOME], F32),
+    "offb": ("sbuf", [128, HOME + BAGS // 16], U16),
     "acc": ("sbuf", [128, NB * BAGS], F32),
     "ps": ("psum", [128, 4096], F32),
 }
@@ -55,7 +58,7 @@ for _t in range(4):
     SCRATCH["off%d" % _t] = ("sbuf", [128, 2 * LIST], U16)
 for _k in range(NB):
     SCRATCH["z%d" % _k] = ("sbuf", [128, ZW], F32)
-SEMAPHORES = ["ldl", "ldx", "ldb", "ldw", "ldr", "vs", "ss", "ps", "gs", "loc", "st", "a0", "a1", "a2", "a3"]
+SEMAPHORES = ["ldl", "ldx", "ldb", "ldw", "ldt", "vs", "ss", "ps", "gs", "loc", "st", "a0", "a1", "a2", "a3"]
 
 
 def rank_program(g, core, T, topo):
@@ -63,16 +66,17 @@ def rank_program(g, core, T, topo):
     if r is None:
         return
     Alu, Copy = AluOpType, ActivationFunctionType.Copy
-    V = g.vector
-    order = sorted(range(1, N // 2), key=lambda x: (topo.host(T.cores[2 * x]) == topo.host(T.cores[0]), -x)) + [0]
-    NCH = len(order)
-    peers = [[2 * (r // 2 ^ x) + m for m in range(2)] for x in order]
-    mem, mate = r % 2, r ^ 1
-    owners = peers[0] + peers[1] + [r] + peers[2] + [mate]
+    V, S = g.vector, g.scalar
+    order = sorted(range(1, N // 2), key=lambda x: (topo.host(T.cores[2 * x]) == topo.host(T.cores[0]), -x))
+    chunks = [[2 * (r // 2 ^ x) + m for m in range(2)] for x in order] + [[r ^ 1], [r]]
+    NCH = len(chunks)
+    start = [CAP * sum(len(c) for c in chunks[:i]) for i in range(NCH + 1)]
+    sums = [0, 1, 4, 2, 3]
+    owners = [s for c in sums for s in chunks[c]]
 
     cnt = {"vs": 0, "ss": 0, "ps": 0, "gs": 0}
     seen = {}
-    queues = {"v": g.vector, "s": g.scalar, "t": g.tensor, "y": g.sync, "g": g}
+    queues = {"v": V, "s": S, "t": g.tensor, "y": g.sync, "g": g}
 
     def need(qn, sem, val):
         if val > seen.get((qn, sem), 0):
@@ -84,24 +88,25 @@ def rank_program(g, core, T, topo):
         cnt[sem] += 1
         return cnt[sem]
 
+    for i, s in enumerate(owners):
+        q = S if i % 2 else g.sync
+        q.dma_start(T.bagg[16 * i:16 * i + 16, :], T.bag[:, LC * s:LC * s + LC]).then_inc(T.sem.ldb, 16)
     for grp in range(2):
         g.sync.dma_start(T.lraw[16 * grp:16 * grp + 16, 0:LIST], T["it"][:, :]).then_inc(T.sem.ldl, 16)
-        g.scalar.dma_start(T.lraw[16 * grp:16 * grp + 16, LIST:2 * LIST], T["it2"][:, :]).then_inc(T.sem.ldl, 16)
-    for i, s in enumerate(owners):
-        q = g.scalar if i % 2 else g.sync
-        q.dma_start(T.bagg[16 * i:16 * i + 16, :], T.bag[:, LC * s:LC * s + LC]).then_inc(T.sem.ldb, 16)
+        S.dma_start(T.lraw[16 * grp:16 * grp + 16, LIST:2 * LIST], T["it2"][:, :]).then_inc(T.sem.ldl, 16)
     g.sync.dma_start(T.exw[:, ZERO:WIN], T.ex[:, :]).then_inc(T.sem.ldx, 16)
     g.sync.dma_start(T.wt[:, :], T.w[:, :]).then_inc(T.sem.ldw, 16)
 
-    def zeros(ap, n):
-        return did("gs", g.iota(ap, [[0, n]], 0, 0, allow_small_or_imprecise_dtypes=True))
+    def ramp(ap, pattern):
+        return did("gs", g.iota(ap, pattern, 0, 0, allow_small_or_imprecise_dtypes=True))
     g_ip = did("gs", g.iota(T.ip[:, :], [[1, 1]], 0, 1))
-    g_io = did("gs", g.iota(T.io1[:, :], [[1, CAP]], 0, 0, allow_small_or_imprecise_dtypes=True))
-    g_du = did("gs", g.iota(T.dumpo[:, :], [[16, LC]], BAGS + 1, 1))
-    g_pt = zeros(T.prt[:, :], BAGS)
-    g_pw = zeros(T.prw[:, BAGS:INV], INV - BAGS)
+    g_io = ramp(T.io1[:, :], [[1, CAP]])
+    did("gs", g.iota(T.bo[:, LC:LW], [[BAGS // 2, 2]], 0, 1))
+    g_du = did("gs", g.iota(T.dumpo[:, :], [[16, LC]], BAGS, 1))
+    g_pw = ramp(T.prw[:, :], [[0, INV]])
+    g_gate = ramp(T.gate[:, :], [[0, 2 * LW], [ZW, 16]])
     for o in range(NB):
-        g_z = zeros(T["z%d" % o][:, 0:SL], SL)
+        g_z = ramp(T["z%d" % o][:, 0:SL], [[0, SL]])
     did("vs", V.memset(T.exw[:, 0:ZERO], 0.0))
     did("vs", V.memset(T.inv[:, :], 0.0))
     need("v", "gs", g_ip)
@@ -112,126 +117,119 @@ def rank_program(g, core, T, topo):
     need("v", "vs", k)
     did("vs", V.tensor_scalar(T.vals[:, :], T.io1[:, :], T.ipf[:, 0:1], None, Alu.add))
 
-    last = [0]
-    steps = []
+    invert = [lambda: V.tensor_scalar(T.pos[:, :], T.bagg[:, :], 2 * BAGS - 1, None, Alu.bitwise_and),
+              lambda: V.tensor_tensor(T.bo[:, 0:LC], T.pos[:, :], T.dumpo[:, :], Alu.min),
+              lambda: V.tensor_copy(T.boff[:, :], T.bo[:, 0:LC]),
+              lambda: V.tensor_copy(T.inv[:, 0:INV].indirect(T.boff[:, :]), T.vals[:, :])]
+    need("v", "ldb", 16 * N)
+    need("v", "gs", g_du)
+    kb, kc, v_off, qd, d = 0, 0, [], 1, 0
+    for x in PRE:
+        if x == "i":
+            need("v", "vs", kb)
+            kb = did("vs", invert.pop(0)())
+        elif x == "c":
+            need("v", "ldl", 64)
+            kc = did("vs", V.tensor_copy(T.lraw[32 * qd:32 * qd + 32, :], T.lraw[0:32, :]))
+            qd += 1
+        elif x == "o":
+            need("v", "vs", kc)
+            t = len(v_off)
+            v_off.append(did("vs", V.tensor_scalar(T["off%d" % t][:, :], T.lraw[:, :], 4.0, float(ZERO + t), Alu.mult, Alu.add)))
+        else:
+            v_tw = did("vs", V.tensor_copy(T.twice[:, d:2 * LW:2], T.bo[:, :]))
+            d += 1
+    need("y", "gs", g_pw)
+    need("y", "vs", kb)
+    for i in range(N):
+        g.sync.dma_start(T.prw[8 + i:8 + i + 15 * N - 14:15, 0:BAGS], T.inv[16 * i:16 * i + N, 0:BAGS]).then_inc(T.sem.ldt, 16)
 
-    def step(f, *waits):
-        def run():
-            for sem, val in waits:
-                need("v", sem, val)
-            need("v", "vs", last[0])
-            last[0] = did("vs", f())
-        steps.append(run)
-
-    def run_steps(n):
-        for f in steps[:n]:
-            f()
-        del steps[:n]
-
-    step(lambda: V.tensor_scalar(T.neg[:, :], T.bagg[:, :], 0, None, Alu.is_lt), ("ldb", 16 * N))
-    step(lambda: V.tensor_tensor(T.dmp[:, :], T.neg[:, :], T.dumpo[:, :], Alu.mult), ("gs", g_du))
-    step(lambda: V.tensor_tensor(T.bo[:, :], T.bagg[:, :], T.dmp[:, :], Alu.add))
-    step(lambda: V.tensor_copy(T.boff[:, :], T.bo[:, :]))
-    step(lambda: V.tensor_copy(T.inv[:, 0:INV].indirect(T.boff[:, 0:LC]), T.vals[:, :]))
-    step(lambda: V.transpose(T.invt[:, :], T.inv[:, 0:BAGS]))
-    step(lambda: V.tensor_tensor(T.pm[:, :], T.invt[:, 0:BAGS:32], T.invt[:, 16:BAGS:32], Alu.max))
-    for a in range(1, 4):
-        p, n = 32 * a - 32, 32 * a
-        step(lambda p=p, n=n: V.tensor_copy(T.prt[n:n + 32, 0:BAGS:32], T.pm[p:p + 32, :]), ("gs", g_pt))
-        to = T.pm[n:n + 32, :] if a < 3 else T.cc[n:n + 32, 2 * HB:2 * HB + NC]
-        step(lambda n=n, to=to: V.tensor_tensor(to, T.prt[n:n + 32, 0:BAGS:32], T.pm[n:n + 32, :], Alu.max))
-    step(lambda: V.tensor_tensor(T.prt[:, 16:BAGS:32], T.prt[:, 0:BAGS:32], T.invt[:, 0:BAGS:32], Alu.max))
-    step(lambda: V.transpose(T.prw[:, 0:BAGS], T.prt[:, :]))
-    step(lambda: V.tensor_copy(T.pv[:, :], T.prw[:, 0:INV].indirect(T.boff[:, 0:LC])), ("gs", g_pw))
-    step(lambda: V.transpose(T.pvt[:, :], T.pv[:, :]))
-
-    def extract():
-        need("v", "vs", last[0])
-        for hh in range(2):
-            last[0] = did("vs", V.tensor_copy(T.cc[:, HB * hh:HB * hh + HB], T.pvt[:, 16 * hh:CAP:32]))
-        need("y", "vs", last[0])
-        for a in range(4):
-            n = 2 * HB + (NC if a == 3 else 0)
-            for hh in range(2):
-                for grp in range(2):
-                    b = RAW * hh + 2 * HB * a
-                    g.sync.dma_start(T.raw[16 * grp:16 * grp + 16, b:b + n],
-                                     T.cc[32 * a + 16 * hh:32 * a + 16 * hh + 16, 0:n]).then_inc(T.sem.ldr, 16)
-
-    def spread():
-        need("v", "ldr", 16 * 16)
-        for hh in range(2):
-            last[0] = did("vs", V.tensor_copy(T.offb[0:32, hh:2 * RAW:2], T.raw[:, RAW * hh:RAW * hh + RAW]))
-
-    def spread_on():
-        need("v", "vs", last[0])
-        for qd in range(1, 4):
-            last[0] = did("vs", V.tensor_copy(T.offb[32 * qd:32 * qd + 32, :], T.offb[0:32, :]))
-
-    need("v", "ldl", 64)
-    for qd in range(1, 4):
-        k = did("vs", V.tensor_copy(T.lraw[32 * qd:32 * qd + 32, :], T.lraw[0:32, :]))
-    run_steps(1)
-    need("v", "vs", k)
-    v_off = []
-    for t in range(4):
-        v_off.append(did("vs", V.tensor_scalar(T["off%d" % t][:, :], T.lraw[:, :], 4.0, float(ZERO + t), Alu.mult, Alu.add)))
-        run_steps(1)
-    run_steps(4)
-
-    s_u = {}
-    need("s", "ldx", 16)
-    for c in range(NCH):
-        l = LC * peers[c][0]
-        for t in range(4):
-            need("s", "vs", v_off[t])
-            b = (4 * c + t) * PAIR
-            s_u[c, t] = did("ss", g.scalar.activation(T.hu[:, b:b + PAIR], T.exw[:, 0:WIN].indirect(T["off%d" % t][:, l:l + 2 * LC]), Copy))
+    s_u = []
     v_h = [0] * NCH
     v_q = [0] * NCH
+    at = [0] * NCH
+    v_w = []
+    last = [0]
 
-    def part(c, t):
+    def items(n, second):
+        c, t = n // 4, n % 4
+        l = second * LIST + LC * chunks[c][0]
+        w = start[c + 1] - start[c]
+        return T.exw[:, 0:WIN].indirect(T["off%d" % t][:, l:l + w // 16]), T.hu[:, 4 * start[c] + t * w:4 * start[c] + (t + 1) * w]
+
+    def part(n):
+        c = n // 4
+        src, out = items(n, 0)
         need("v", "ldx", 16)
-        need("v", "vs", v_off[t])
-        need("v", "ss", s_u[c, t])
-        b = (4 * c + t) * PAIR
-        l = LIST + LC * peers[c][0]
-        v_h[c] = did("vs", V.tensor_tensor(T.h[:, 4 * c * PAIR + t:4 * (c + 1) * PAIR:4],
-                                           T.exw[:, 0:WIN].indirect(T["off%d" % t][:, l:l + 2 * LC]), T.hu[:, b:b + PAIR], Alu.add))
+        need("v", "vs", v_off[n % 4])
+        if n < SELF:
+            need("v", "vs", did("vs", V.tensor_copy(out, src)))
+        else:
+            need("s", "ldx", 16)
+            need("s", "vs", v_off[n % 4])
+            need("v", "ss", did("ss", S.activation(out, src, Copy)))
+        v_h[c] = did("vs", V.tensor_tensor(T.h[:, 4 * start[c] + n % 4:4 * start[c + 1]:4], items(n, 1)[0], out, Alu.add))
 
     def quant(c):
         need("v", "vs", v_h[c])
-        a, b = c * PAIR, (c + 1) * PAIR
-        v_q[c] = did("vs", V.quantize_mx(T.q[:, a:b], T.qsc[:, a:b], T.h[:, 4 * a:4 * b]))
+        b = start[c + 1]
+        a = min(start[c], b - TILE)
+        o = a if a == start[c] else QW - TILE * (NCH - c)
+        at[c] = o + start[c] - a
+        v_q[c] = did("vs", V.quantize_mx(T.q[:, o:o + b - a], T.qsc[:, o:o + b - a], T.h[:, 4 * a:4 * b]))
 
-    for t in range(4):
-        part(0, t)
-        run_steps(1)
-    run_steps(1)
-    quant(0)
-    for t in range(3):
-        part(1, t)
-        run_steps(1)
-    part(1, 3)
-    extract()
-    part(2, 0)
-    quant(1)
-    for t in range(1, 4):
-        part(2, t)
-    part(3, 0)
-    quant(2)
-    need("v", "ldw", 16)
-    v_w = did("vs", V.quantize_mx(T.wq[:, :], T.wsc[:, :], T.wt[:, :]))
-    for t in range(1, 4):
-        part(3, t)
-    spread()
-    quant(3)
-    spread_on()
+    def rows():
+        need("s", "ldt", 16 * N)
+        need("s", "vs", v_tw)
+        last[0] = did("ss", S.activation(T.pv[:, :], T.prw[:, 0:INV].indirect(T.twice[:, :]), Copy))
+
+    def turn():
+        need("v", "ss", last[0])
+        last[0] = did("vs", V.transpose(T.pvt[:, :], T.pv[:, :]))
+
+    def scan():
+        need("v", "gs", g_gate)
+        need("v", "vs", last[0])
+        last[0] = did("vs", V.tensor_tensor_scan(T.run[:, :], T.gate[:, :], T.pvt[:, :], 0.0, Alu.min, Alu.max))
+
+    def extract():
+        need("s", "vs", last[0])
+        for h in range(2):
+            did("ss", S.activation(T.raw[:, LW * h:LW * h + LC], T.run[:, 16 * h + 7:32 * LC:32], Copy))
+            last[0] = did("ss", S.activation(T.raw[:, LW * h + LC:LW * h + LW], T.run[:, 32 * LC + 16 * h + 15:PV:32], Copy))
+
+    def collect():
+        need("s", "ss", last[0])
+        for qd in range(1, 4):
+            last[0] = did("ss", S.activation(T.raw[0:32, 2 * LW * qd:2 * LW * (qd + 1)], T.raw[32 * qd:32 * qd + 32, 0:2 * LW], Copy))
+
+    def spread():
+        need("s", "ss", last[0])
+        for qd in range(1, 4):
+            last[0] = did("ss", S.activation(T.raw[32 * qd:32 * qd + 32, :], T.raw[0:32, :], Copy))
+
+    def weights():
+        need("v", "ldw", 16)
+        v_w.append(did("vs", V.quantize_mx(T.wq[:, :], T.wsc[:, :], T.wt[:, :])))
+
+    behind = [(ROWS_AT, rows), (T_AT, turn), (T_AT + 1, scan), (X_AT, extract), (X_AT + 2, collect), (X_AT + 4, spread), (W_AT, weights)]
+    for n in range(4 * NCH):
+        part(n)
+        if n % 4 == 0 and n:
+            quant(n // 4 - 1)
+        for m, f in behind:
+            if min(m, 4 * NCH) == n + 1:
+                f()
+    need("v", "ss", last[0])
+    v_l = did("vs", V.tensor_copy(T.offb[:, 0:HOME], T.raw[:, :]))
+    for kk in range(2):
+        v_home = did("vs", V.tensor_copy(T.offb[:, HOME + N * kk:HOME + N * kk + N], T.raw[:, LC + kk:HOME:LW]))
+    quant(NCH - 1)
 
     loc = 0
     arr = []
-    for c in range(NCH):
-        dests = [d for d in peers[c] if d != r]
+    for c in range(NCH - 1):
+        dests = chunks[c]
         need("g", "vs", v_q[c])
         for kind in range(2):
             tr, tot = [], 0
@@ -240,8 +238,8 @@ def rank_program(g, core, T, topo):
                 eng = topo.engines(core, dst)
                 n = len(eng) // len(dests)
                 rid, pnc = topo.addr(dst, core)
-                a = c * PAIR + CAP * (d % 2)
-                b = c * PAIR + (CAP * mem if c < NCH - 1 else 0)
+                a = at[c] + CAP * i
+                b = start[c] + CAP * (r % len(dests))
                 if kind == 0:
                     src, out = T.q[:, a:a + CAP].bitcast(dt.uint8), T.lq[:, b:b + CAP].bitcast(dt.uint8)
                 else:
@@ -253,61 +251,62 @@ def rank_program(g, core, T, topo):
             loc += tot
         arr.append(2 * tot)
 
-    need("t", "vs", v_w)
-    use = 0
     bank_free = [0] * 8
+    use = [0]
     z_in = {}
-    own = (NCH - 1) * PAIR + CAP * mem
-    own_first = min(own, N * CAP - 128)
-    mate_first = (NCH - 1) * PAIR + CAP - 128
-    stages = [(T.lq, T.lsc, 0, 0, PAIR, 0, "a0", arr[0]),
-              (T.lq, T.lsc, PAIR, 0, PAIR, 2, "a1", arr[1]),
-              (T.q, T.qsc, own_first, own - own_first, CAP, 4, "vs", v_q[3]),
-              (T.lq, T.lsc, 2 * PAIR, 0, PAIR, 5, "a2", arr[2]),
-              (T.lq, T.lsc, mate_first, 128 - CAP, CAP, 7, "a3", arr[3])]
-    for src, ssc, first, lo, width, place, sem, val in stages:
-        need("t", sem, val)
-        n = max(128, width)
+    chain = [v_l] * NB
+
+    def product(st, o):
+        c = sums[st]
+        place = sum(len(chunks[x]) for x in sums[:st])
+        width = start[c + 1] - start[c]
+        n = max(TILE, width)
+        need("t", "vs", v_w[0])
+        if c < NCH - 1:
+            src, ssc, first = T.lq, T.lsc, start[c + 1] - n
+            need("t", "a%d" % c, arr[c])
+        else:
+            src, ssc, first = T.q, T.qsc, QW - n
+            need("t", "vs", v_q[c])
+        bk = use[0] % 8
+        use[0] += 1
+        need("t", "ss", bank_free[bk])
+        p = did("ps", g.tensor.matmul_mx(T.ps[:, 512 * bk:512 * bk + n], T.wq[:, 128 * o:128 * o + 128], T.wsc[:, 128 * o:128 * o + 128],
+                                         src[:, first:first + n], ssc[:, first:first + n], True, True))
+        need("s", "ps", p)
+        b = SL + CAP * place
+        bank_free[bk] = did("ss", S.activation(T["z%d" % o][:, b:b + width], T.ps[:, 512 * bk + n - width:512 * bk + n], Copy))
+        for i in range(width // CAP):
+            z_in[place + i, o] = bank_free[bk]
+
+    for st in range(NCH):
         for o in range(NB):
-            bk = use % 8
-            use += 1
-            need("t", "ss", bank_free[bk])
-            p = did("ps", g.tensor.matmul_mx(T.ps[:, 512 * bk:512 * bk + n], T.wq[:, 128 * o:128 * o + 128], T.wsc[:, 128 * o:128 * o + 128],
-                                             src[:, first:first + n], ssc[:, first:first + n], True, True))
-            need("s", "ps", p)
-            b = SL + CAP * place
-            k = did("ss", g.scalar.activation(T["z%d" % o][:, b:b + width], T.ps[:, 512 * bk + lo:512 * bk + lo + width], Copy))
-            bank_free[bk] = k
-            for i in range(width // CAP):
-                z_in[place + i, o] = k
+            product(st, o)
 
-    chain = [0] * NB
-    for i in range(1, N):
-        for o in (0, 2, 1) if i == N - 1 else range(NB):
-            z = T["z%d" % o]
-            b = SL + CAP * i
-            need("v", "gs", g_z)
-            need("v", "vs", max(chain[o], last[0]))
-            need("v", "ss", z_in[i, o])
-            chain[o] = did("vs", V.tensor_tensor(z[:, b:b + CAP], z[:, 0:b].indirect(T.offb[:, LC * i:LC * i + LC]), z[:, b:b + CAP], Alu.add))
+    need("v", "gs", g_z)
+    need("s", "gs", g_z)
+    for i, o in [(i, o) for i in range(1, TAIL[0][0]) for o in range(NB)] + TAIL:
+        b = SL + CAP * i
+        z = T["z%d" % o]
+        need("v", "vs", chain[o])
+        need("v", "ss", z_in[i, o])
+        chain[o] = did("vs", V.tensor_tensor(z[:, b:b + CAP], z[:, 0:b].indirect(T.offb[:, LW * i:LW * i + LC]), z[:, b:b + CAP], Alu.add))
 
-    for o in (0, 2, 1):
-        y = T.acc[:, BAGS * o:BAGS * (o + 1)]
-        win = T["z%d" % o][:, 0:ZW].indirect(T.offb[:, HOME:HOME + BAGS // 16])
-        if o == 2:
-            need("v", "vs", chain[o])
-            k = did("vs", V.tensor_copy(y, win))
-            need("y", "vs", k)
+    pieces = PIECES
+    for qn, o, a, b in pieces:
+        y = T.acc[:, BAGS * o + a:BAGS * o + b]
+        win = T["z%d" % o][:, 0:ZW].indirect(T.offb[:, HOME + a // 16:HOME + b // 16])
+        need(qn, "vs", max(chain[o], v_home))
+        if qn == "v":
+            need("y", "vs", did("vs", V.tensor_copy(y, win)))
             q = g.sync
         else:
-            need("s", "gs", g_z)
-            need("s", "vs", chain[o])
-            k = did("ss", g.scalar.activation(y, win, Copy))
-            q = g.scalar if o == 1 else g.sync
+            k = did("ss", S.activation(y, win, Copy))
+            q = S if o == 1 else g.sync
             need("s" if o == 1 else "y", "ss", k)
-        q.dma_start(T.y[:, BAGS * o:BAGS * (o + 1)], y).then_inc(T.sem.st, 16)
+        q.dma_start(T.y[:, BAGS * o + a:BAGS * o + b], y).then_inc(T.sem.st, 16)
 
     need("g", "loc", loc)
     for sem in ("gs", "vs", "ss", "ps"):
         need("g", sem, cnt[sem])
-    need("g", "st", 16 * NB)
+    need("g", "st", 16 * len(pieces))

@@ -1,312 +1,315 @@
 from concourse.bass import DstId, RemoteDMATransfer
-from concourse.mybir import dt, AluOpType, ActivationFunctionType
+from concourse.mybir import dt, AluOpType, ActivationFunctionType, AxisListType
 
 N, CAP, BAGS, NB, ITEMS = 8, 96, 256, 3, 512
 TILE = 128
+PAD = TILE - CAP
+PAIR = 2 * CAP
+NP = N // 2
 LC = CAP // 16
-LIST = N * LC
 ZERO = 16
 WIN = ZERO + 4 * ITEMS
 INV = 464
 SL = 8
 ZW = SL + N * CAP
-LW = LC + 2
+HC = BAGS // 16 // NP
+LW = LC + HC
 PV = 32 * LW
-HOME = N * LW
-QW = (N - 2) * CAP + 2 * TILE
-ROWS_AT, T_AT, X_AT, W_AT = 8, 10, 18, 13
-SELF = 1
-PRE = "icccioooiotti"
-TAIL = [(7, 0), (7, 2), (7, 1)]
-PIECES = [("s", 0, 0, BAGS), ("v", 2, 0, BAGS), ("s", 1, 0, BAGS)]
+HW = PAD + N * CAP
+QW = HW + 2 * TILE
+CH = "MABPS"
+QUAD = "AOBP"
+HALVES = {"A": "CD", "B": "EF", "O": "SM", "P": "XY"}
+YQ = "it0 it1 b0 ex w"
+XQ = "jt0 jt1 b1"
+VP = "zx zh i1 i2 o0 pos o1 o2 o3 bo boff"
+VQ = "p00 p01 p02 p03 scat q0 p10 p11 p12 p13 p20 q1 p21 p22 p23 p30 q2 p31 p32 p33 turn q3 red w2 w0 w1 p40 p41 p42 p43 ls q4 lx ly"
+SQ = "i3 home vals f00 f01 f02 f03 f10 f11 F12 F20 F22 F30 F32 rows f40 twice f41 f42 f43 collect spread"
+VS = "lM2 lM0 lM1 aS2 aS0 aS1 lB0 lB1 lX0 aB2 lX1 aY0 lX2 aY1 lY2 y0 y1 y2"
+SS = "eA2 eM2 eA0 eM0 eA1 eM1 gS2 gS0 gS1 eB0 eB1 gB2 eX0 eX1 gY0 eX2 gY1 eY2 x0 x1 x2"
+GQ = "c0 s0 c1 s1 c2 s2 c3x s3 c3y"
+TQ = "A2 M2 A0 M0 A1 M1 B0 S2 S0 B1 S1 X0 X1 X2 B2 Y2 Y0 Y1"
 F32, BF, I32, U16 = "float32", "bfloat16", "int32", "uint16"
 SCRATCH = {
     "exw": ("sbuf", [128, WIN], BF),
     "wt": ("sbuf", [128, 512 * NB], BF),
     "wq": ("sbuf", [128, 128 * NB], "float8_e4m3fn_x4"),
     "wsc": ("sbuf", [128, 128 * NB], "uint8"),
-    "lraw": ("sbuf", [128, 2 * LIST], I32),
+    "lraw": ("sbuf", [128, N, 2 * LC], I32),
+    "off": ("sbuf", [128, N, 8 * LC], U16),
     "hu": ("sbuf", [128, 4 * N * CAP], BF),
-    "h": ("sbuf", [128, 4 * N * CAP], BF),
+    "h": ("sbuf", [128, 4 * HW], BF),
     "q": ("sbuf", [128, QW], "float8_e4m3fn_x4"),
     "qsc": ("sbuf", [128, QW], "uint8"),
     "lq": ("sbuf", [128, (N - 1) * CAP], "float8_e4m3fn_x4"),
     "lsc": ("sbuf", [128, (N - 1) * CAP], "uint8"),
-    "bagg": ("sbuf", [128, LC], I32),
+    "bagg": ("sbuf", [128, (N - 1) * LC], I32),
     "pos": ("sbuf", [128, LC], I32),
     "dumpo": ("sbuf", [128, LC], I32),
-    "bo": ("sbuf", [128, LW], I32),
-    "boff": ("sbuf", [128, LC], U16),
-    "twice": ("sbuf", [128, 2 * LW], U16),
+    "bo": ("sbuf", [128, LW], F32),
+    "ib": ("sbuf", [128, HC], F32),
+    "boff": ("sbuf", [128, LW], U16),
     "ip": ("sbuf", [128, 1], I32),
-    "ip2": ("sbuf", [128, 1], I32),
-    "ipf": ("sbuf", [128, 1], F32),
+    "ipi": ("sbuf", [128, 3], I32),
+    "ipf": ("sbuf", [128, 6], F32),
     "io1": ("sbuf", [128, CAP], F32),
     "vals": ("sbuf", [128, CAP], F32),
     "inv": ("sbuf", [128, INV], F32),
     "prw": ("sbuf", [128, INV], F32),
-    "gate": ("sbuf", [128, PV], F32),
-    "pv": ("sbuf", [128, PV], F32),
-    "pvt": ("sbuf", [128, PV], F32),
-    "run": ("sbuf", [128, PV], F32),
-    "raw": ("sbuf", [128, HOME], F32),
-    "offb": ("sbuf", [128, HOME + BAGS // 16], U16),
+    "once": ("sbuf", [128, 16 * LW], F32),
+    "pv": ("sbuf", [128, LW, 32], F32),
+    "pvt": ("sbuf", [128, 2 * LW, 16], F32),
+    "raw": ("sbuf", [128, NP, 2 * LW], F32),
+    "offs": ("sbuf", [128, NP, 2 * LC], U16),
+    "offh": ("sbuf", [128, 2, NP * HC], U16),
+    "tmp": ("sbuf", [128, NB * NP * PAIR], F32),
+    "half": ("sbuf", [128, NB * BAGS], F32),
     "acc": ("sbuf", [128, NB * BAGS], F32),
     "ps": ("psum", [128, 4096], F32),
 }
-for _t in range(4):
-    SCRATCH["off%d" % _t] = ("sbuf", [128, 2 * LIST], U16)
 for _k in range(NB):
     SCRATCH["z%d" % _k] = ("sbuf", [128, ZW], F32)
-SEMAPHORES = ["ldl", "ldx", "ldb", "ldw", "ldt", "vs", "ss", "ps", "gs", "loc", "st", "a0", "a1", "a2", "a3"]
+SEMAPHORES = ["ldl", "ldx", "ldb", "ldw", "ldt", "vs", "ss", "ps", "gs", "loc", "st"] + ["a%d%s" % (_c, _h) for _c in range(5) for _h in "xy"]
 
 
 def rank_program(g, core, T, topo):
     r = T.rank_of(core)
     if r is None:
         return
-    Alu, Copy = AluOpType, ActivationFunctionType.Copy
+    Alu, Copy, Same = AluOpType, ActivationFunctionType.Copy, ActivationFunctionType.Identity
     V, S = g.vector, g.scalar
-    order = sorted(range(1, N // 2), key=lambda x: (topo.host(T.cores[2 * x]) == topo.host(T.cores[0]), -x))
-    chunks = [[2 * (r // 2 ^ x) + m for m in range(2)] for x in order] + [[r ^ 1], [r]]
+    order = sorted(range(1, NP), key=lambda x: (topo.host(T.cores[2 * x]) == topo.host(T.cores[0]), -x))
+    who = {k: [2 * (r // 2 ^ x) + m for m in range(2)] for k, x in zip("ABP", order)}
+    who.update(M=[r ^ 1], S=[r])
+    chunks = [who[k] for k in CH]
     NCH = len(chunks)
     start = [CAP * sum(len(c) for c in chunks[:i]) for i in range(NCH + 1)]
-    sums = [0, 1, 4, 2, 3]
-    owners = [s for c in sums for s in chunks[c]]
+    pairs = [[r, r ^ 1] if k == "O" else who[k] for k in QUAD]
+    lands = [(k.replace("O", "M"), h) for k in QUAD for h in "xy" if k + h != "Ox"]
+    plan = {"v": " ".join([VP, VQ, VS]).split(), "s": (SQ + " " + SS).split(), "t": ["mm" + x for x in TQ.split()]}
 
-    cnt = {"vs": 0, "ss": 0, "ps": 0, "gs": 0}
     seen = {}
     queues = {"v": V, "s": S, "t": g.tensor, "y": g.sync, "g": g}
+    sems = {"v": "vs", "s": "ss", "t": "ps", "g": "gs"}
+    cnt = {"v": 0, "s": 0, "t": 0, "g": 0}
 
     def need(qn, sem, val):
         if val > seen.get((qn, sem), 0):
             queues[qn].wait_ge(T.sem[sem], val)
             seen[(qn, sem)] = val
 
-    def did(sem, ins):
-        ins.then_inc(T.sem[sem], 1)
-        cnt[sem] += 1
-        return cnt[sem]
+    def did(qn, ins):
+        ins.then_inc(T.sem[sems[qn]], 1)
+        cnt[qn] += 1
+        return cnt[qn]
 
-    for i, s in enumerate(owners):
-        q = S if i % 2 else g.sync
-        q.dma_start(T.bagg[16 * i:16 * i + 16, :], T.bag[:, LC * s:LC * s + LC]).then_inc(T.sem.ldb, 16)
-    for grp in range(2):
-        g.sync.dma_start(T.lraw[16 * grp:16 * grp + 16, 0:LIST], T["it"][:, :]).then_inc(T.sem.ldl, 16)
-        S.dma_start(T.lraw[16 * grp:16 * grp + 16, LIST:2 * LIST], T["it2"][:, :]).then_inc(T.sem.ldl, 16)
-    g.sync.dma_start(T.exw[:, ZERO:WIN], T.ex[:, :]).then_inc(T.sem.ldx, 16)
-    g.sync.dma_start(T.wt[:, :], T.w[:, :]).then_inc(T.sem.ldw, 16)
+    loads = {"ex": (T.exw[:, ZERO:WIN], T.ex[:, :], "ldx"), "w": (T.wt[:, :], T.w[:, :], "ldw")}
+    for i in range(2):
+        first = LC * ((r + i) % 2)
+        loads["b%d" % i] = (T.bagg[16 * i:16 * i + 16, :], T.bag[:, first:first + (N - 1) * LC], "ldb")
+        loads["it%d" % i] = (T.lraw[16 * i:16 * i + 16, 0:NP, :], T["it"][:, :], "ldl")
+        loads["jt%d" % i] = (T.lraw[16 * i:16 * i + 16, NP:N, :], T["it2"][:, :], "ldl")
+    for q, names in ((g.sync, YQ), (S, XQ)):
+        for name in names.split():
+            out, in_, sem = loads[name]
+            q.dma_start(out, in_).then_inc(T.sem[sem], 16)
 
-    def ramp(ap, pattern):
-        return did("gs", g.iota(ap, pattern, 0, 0, allow_small_or_imprecise_dtypes=True))
-    g_ip = did("gs", g.iota(T.ip[:, :], [[1, 1]], 0, 1))
-    g_io = ramp(T.io1[:, :], [[1, CAP]])
-    did("gs", g.iota(T.bo[:, LC:LW], [[BAGS // 2, 2]], 0, 1))
-    g_du = did("gs", g.iota(T.dumpo[:, :], [[16, LC]], BAGS, 1))
+    def ramp(ap, pattern, base=0):
+        return ("gs", did("g", g.iota(ap, pattern, base, 0, allow_small_or_imprecise_dtypes=True)))
+    g_ip = ("gs", did("g", g.iota(T.ip[:, :], [[1, 1]], 0, 1)))
+    ramp(T.ib[:, :], [[16, HC]])
+    g_io = ramp(T.io1[:, :], [[1, CAP]], SL)
+    g_du = ("gs", did("g", g.iota(T.dumpo[:, :], [[16, LC]], BAGS, 1)))
+    g_inv = ramp(T.inv[:, :], [[0, INV]])
     g_pw = ramp(T.prw[:, :], [[0, INV]])
-    g_gate = ramp(T.gate[:, :], [[0, 2 * LW], [ZW, 16]])
     for o in range(NB):
         g_z = ramp(T["z%d" % o][:, 0:SL], [[0, SL]])
-    did("vs", V.memset(T.exw[:, 0:ZERO], 0.0))
-    did("vs", V.memset(T.inv[:, :], 0.0))
-    need("v", "gs", g_ip)
-    k = did("vs", V.tensor_scalar(T.ip2[:, :], T.ip[:, :], 4, None, Alu.arith_shift_right))
-    need("v", "vs", k)
-    k = did("vs", V.tensor_scalar(T.ipf[:, :], T.ip2[:, :], float(CAP), float(SL), Alu.mult, Alu.add))
-    need("v", "gs", g_io)
-    need("v", "vs", k)
-    did("vs", V.tensor_scalar(T.vals[:, :], T.io1[:, :], T.ipf[:, 0:1], None, Alu.add))
 
-    invert = [lambda: V.tensor_scalar(T.pos[:, :], T.bagg[:, :], 2 * BAGS - 1, None, Alu.bitwise_and),
-              lambda: V.tensor_tensor(T.bo[:, 0:LC], T.pos[:, :], T.dumpo[:, :], Alu.min),
-              lambda: V.tensor_copy(T.boff[:, :], T.bo[:, 0:LC]),
-              lambda: V.tensor_copy(T.inv[:, 0:INV].indirect(T.boff[:, :]), T.vals[:, :])]
-    need("v", "ldb", 16 * N)
-    need("v", "gs", g_du)
-    kb, kc, v_off, qd, d = 0, 0, [], 1, 0
-    for x in PRE:
-        if x == "i":
-            need("v", "vs", kb)
-            kb = did("vs", invert.pop(0)())
-        elif x == "c":
-            need("v", "ldl", 64)
-            kc = did("vs", V.tensor_copy(T.lraw[32 * qd:32 * qd + 32, :], T.lraw[0:32, :]))
-            qd += 1
-        elif x == "o":
-            need("v", "vs", kc)
-            t = len(v_off)
-            v_off.append(did("vs", V.tensor_scalar(T["off%d" % t][:, :], T.lraw[:, :], 4.0, float(ZERO + t), Alu.mult, Alu.add)))
-        else:
-            v_tw = did("vs", V.tensor_copy(T.twice[:, d:2 * LW:2], T.bo[:, :]))
-            d += 1
-    need("y", "gs", g_pw)
-    need("y", "vs", kb)
-    for i in range(N):
-        g.sync.dma_start(T.prw[8 + i:8 + i + 15 * N - 14:15, 0:BAGS], T.inv[16 * i:16 * i + N, 0:BAGS]).then_inc(T.sem.ldt, 16)
+    steps = {}
 
-    s_u = []
-    v_h = [0] * NCH
-    v_q = [0] * NCH
-    at = [0] * NCH
-    v_w = []
-    last = [0]
+    def step(name, after, *calls):
+        steps[name] = (after, calls)
 
-    def items(n, second):
-        c, t = n // 4, n % 4
-        l = second * LIST + LC * chunks[c][0]
+    def copy(out, in_):
+        return lambda: S.activation(out, in_, Copy)
+
+    def scal(out, in_, *ops):
+        return lambda: V.tensor_scalar(out, in_, *ops)
+
+    def cast(out, in_):
+        return lambda: V.tensor_copy(out, in_)
+
+    step("zx", [], lambda: V.memset(T.exw[:, 0:ZERO], 0.0))
+    step("zh", [], lambda: V.memset(T.h[:, 0:4 * PAD], 0.0))
+    step("i1", [g_ip], scal(T.ipi[:, 0:1], T.ip[:, :], 4, None, Alu.arith_shift_right), scal(T.ipi[:, 1:2], T.ip[:, :], 5, None, Alu.arith_shift_right),
+         scal(T.ipi[:, 2:3], T.ip[:, :], 15, None, Alu.bitwise_and))
+    step("i2", ["i1"], cast(T.ipf[:, 0:3], T.ipi[:, :]))
+    grp, quad, row, bag0, before, slot0 = [T.ipf[:, k:k + 1] for k in range(6)]
+    step("i3", ["i2"], lambda: S.activation(slot0, grp, Copy, scale=float(CAP)), lambda: S.activation(bag0, quad, Same, bias=row, scale=16.0 * HC),
+         lambda: S.activation(before, row, ActivationFunctionType.Sign, bias=quad, scale=-1.0))
+    step("vals", ["i3", g_io], lambda: S.activation(T.vals[:, :], T.io1[:, :], Same, bias=slot0))
+    step("home", ["i3", g_io], lambda: S.activation(T.bo[:, LC:LW], T.ib[:, :], Same, bias=bag0))
+    step("o0", [("ldl", 64)], *[scal(T.off[32 * a:32 * a + 32, :, 0:2 * LC], T.lraw[0:32, :, :], 4.0, float(ZERO), Alu.mult, Alu.add) for a in range(4)])
+    for t in range(1, 4):
+        step("o%d" % t, ["o0"], scal(T.off[:, :, 2 * LC * t:2 * LC * (t + 1)], T.off[:, :, 0:2 * LC], float(t), None, Alu.add))
+    step("pos", [("ldb", 32)], *[scal(T.pos[32 * a:32 * a + 32, :], T.bagg[0:32, LC * min(p):LC * min(p) + LC], 2 * BAGS - 1, None, Alu.bitwise_and)
+                                 for a, p in enumerate(pairs)])
+    step("bo", ["pos", g_du], lambda: V.tensor_tensor(T.bo[:, 0:LC], T.pos[:, :], T.dumpo[:, :], Alu.min))
+    step("boff", ["bo", "home"], cast(T.boff[:, :], T.bo[:, :]))
+    step("scat", ["boff", "vals", g_inv], cast(T.inv[:, 0:INV].indirect(T.boff[:, 0:LC]), T.vals[:, :]))
+
+    def items(c, t, second, n=1):
+        d = chunks[c][0]
+        l = 2 * LC * t + LC * (d % 2)
+        return T.exw[:, 0:WIN].indirect(T.off[:, second * NP + d // 2, l:l + n * LC * len(chunks[c])])
+
+    def parts(c, t):
         w = start[c + 1] - start[c]
-        return T.exw[:, 0:WIN].indirect(T["off%d" % t][:, l:l + w // 16]), T.hu[:, 4 * start[c] + t * w:4 * start[c] + (t + 1) * w]
-
-    def part(n):
-        c = n // 4
-        src, out = items(n, 0)
-        need("v", "ldx", 16)
-        need("v", "vs", v_off[n % 4])
-        if n < SELF:
-            need("v", "vs", did("vs", V.tensor_copy(out, src)))
-        else:
-            need("s", "ldx", 16)
-            need("s", "vs", v_off[n % 4])
-            need("v", "ss", did("ss", S.activation(out, src, Copy)))
-        v_h[c] = did("vs", V.tensor_tensor(T.h[:, 4 * start[c] + n % 4:4 * start[c + 1]:4], items(n, 1)[0], out, Alu.add))
+        u = T.hu[:, 4 * start[c] + t * w:4 * start[c] + (t + 1) * w]
+        one, two = "f%d%d" % (c, t), "F%d%d" % (c, t - t % 2)
+        step(one, [("ldx", 16), "zx", "o%d" % t], (cast if one in plan["v"] else copy)(u, items(c, t, 0)))
+        if t % 2 == 0 and two in plan["s"]:
+            step(two, [("ldx", 16), "zx", "o%d" % (t + 1)], copy(T.hu[:, 4 * start[c] + t * w:4 * start[c] + (t + 2) * w], items(c, t, 0, 2)))
+        step("p%d%d" % (c, t), [two if two in plan["s"] else one, "o%d" % t],
+             lambda: V.tensor_tensor(T.h[:, 4 * (PAD + start[c]) + t:4 * (PAD + start[c + 1]):4], items(c, t, 1), u, Alu.add))
 
     def quant(c):
-        need("v", "vs", v_h[c])
-        b = start[c + 1]
-        a = min(start[c], b - TILE)
-        o = a if a == start[c] else QW - TILE * (NCH - c)
-        at[c] = o + start[c] - a
-        v_q[c] = did("vs", V.quantize_mx(T.q[:, o:o + b - a], T.qsc[:, o:o + b - a], T.h[:, 4 * a:4 * b]))
+        b = PAD + start[c + 1]
+        a = min(PAD + start[c], b - TILE)
+        o = HW + TILE * "MS".index(CH[c]) if CH[c] in "MS" else a
+        step("q%d" % c, ["p%d%d" % (x, t) for t in range(4) for x in range(max(0, c - (a < PAD + start[c])), c + 1)] + ["zh"] * (a < PAD), lambda: V.quantize_mx(T.q[:, o:o + b - a], T.qsc[:, o:o + b - a], T.h[:, 4 * a:4 * b]))
 
-    def rows():
-        need("s", "ldt", 16 * N)
-        need("s", "vs", v_tw)
-        last[0] = did("ss", S.activation(T.pv[:, :], T.prw[:, 0:INV].indirect(T.twice[:, :]), Copy))
+    def weights(o):
+        step("w%d" % o, [("ldw", 16)], lambda: V.quantize_mx(T.wq[:, 128 * o:128 * o + 128], T.wsc[:, 128 * o:128 * o + 128], T.wt[:, 512 * o:512 * o + 512]))
 
-    def turn():
-        need("v", "ss", last[0])
-        last[0] = did("vs", V.transpose(T.pvt[:, :], T.pv[:, :]))
+    for c in range(NCH):
+        quant(c)
+        for t in range(4):
+            parts(c, t)
+    for o in range(NB):
+        weights(o)
 
-    def scan():
-        need("v", "gs", g_gate)
-        need("v", "vs", last[0])
-        last[0] = did("vs", V.tensor_tensor_scan(T.run[:, :], T.gate[:, :], T.pvt[:, :], 0.0, Alu.min, Alu.max))
+    step("rows", [("ldt", 16 * N), "boff", "i3"],
+         lambda: S.activation(T.once[:, 0:CAP], T.prw[:, 0:INV].indirect(T.boff[:, 0:LC]), Same, scale=before),
+         copy(T.once[:, CAP:16 * LW], T.prw[:, 0:INV].indirect(T.boff[:, LC:LW])))
+    step("twice", ["rows"], *[copy(T.pv[:, :, 16 * d:16 * d + 16], T.once[:, :]) for d in range(2)])
+    step("turn", ["twice"], lambda: V.transpose(T.pvt[:, :, :], T.pv[:, :, :]))
+    step("red", ["turn"], lambda: V.tensor_reduce(T.raw[:, 0, :], T.pvt[:, :, 0:NP], AxisListType.X, Alu.max))
+    step("collect", ["red"], *[copy(T.raw[0:32, a, :], T.raw[32 * a:32 * a + 32, 0, :]) for a in range(1, NP)])
+    step("spread", ["collect"], *[copy(T.raw[32 * a:32 * a + 32, :, :], T.raw[0:32, :, :]) for a in range(1, NP)])
+    step("ls", ["spread"], *[cast(T.offs[:, :, LC * h:LC * (h + 1)], T.raw[:, :, h:2 * LC:2]) for h in range(2)])
+    step("lx", ["spread"], cast(T.offh[:, 0, :], T.raw[:, :, 2 * LC:2 * LW:2]))
+    step("ly", ["spread"], cast(T.offh[:, 1, :], T.raw[:, :, 2 * LC + 1:2 * LW:2]))
 
-    def extract():
-        need("s", "vs", last[0])
-        for h in range(2):
-            did("ss", S.activation(T.raw[:, LW * h:LW * h + LC], T.run[:, 16 * h + 7:32 * LC:32], Copy))
-            last[0] = did("ss", S.activation(T.raw[:, LW * h + LC:LW * h + LW], T.run[:, 32 * LC + 16 * h + 15:PV:32], Copy))
+    sends, arrive = [], {}
+    for x in GQ.split():
+        to = [(int(y[0]), d) for y in x[1:].split("+") for d in chunks[int(y[0])] if y[1:] in ("", "xy"[(r ^ d) % 2])]
+        to.sort(key=lambda cd: (cd[0], (r ^ cd[1]) % 2))
+        eng = topo.engines(core, T.cores[to[0][1]])
+        n = [len(eng) // (1 << (len(to) - 1).bit_length())] * len(to)
+        n[0] += len(eng) - sum(n)
+        sends.append((x[0], [(c, d, eng[sum(n[:i]):sum(n[:i + 1])]) for i, (c, d) in enumerate(to)]))
+        for i, (c, d) in enumerate(to):
+            sem = "a%d%s" % (c, "xy"[(r ^ d) % 2])
+            arrive[sem] = arrive.get(sem, 0) + n[i]
 
-    def collect():
-        need("s", "ss", last[0])
-        for qd in range(1, 4):
-            last[0] = did("ss", S.activation(T.raw[0:32, 2 * LW * qd:2 * LW * (qd + 1)], T.raw[32 * qd:32 * qd + 32, 0:2 * LW], Copy))
+    known = plan["v"] + plan["s"] + plan["t"]
 
-    def spread():
-        need("s", "ss", last[0])
-        for qd in range(1, 4):
-            last[0] = did("ss", S.activation(T.raw[32 * qd:32 * qd + 32, :], T.raw[0:32, :], Copy))
+    def pick(kinds, k, h, o):
+        return [x + u + str(o) for x in kinds for u in (k, HALVES[k]["xy".index(h)]) if x + u + str(o) in known][0]
 
-    def weights():
-        need("v", "ldw", 16)
-        v_w.append(did("vs", V.quantize_mx(T.wq[:, :], T.wsc[:, :], T.wt[:, :])))
+    def upto(n, o):
+        return T["z%d" % o][:, 0:SL + CAP * n], [pick("lae", QUAD[i // 2], "xy"[i % 2], o) for i in range(n)]
 
-    behind = [(ROWS_AT, rows), (T_AT, turn), (T_AT + 1, scan), (X_AT, extract), (X_AT + 2, collect), (X_AT + 4, spread), (W_AT, weights)]
-    for n in range(4 * NCH):
-        part(n)
-        if n % 4 == 0 and n:
-            quant(n // 4 - 1)
-        for m, f in behind:
-            if min(m, 4 * NCH) == n + 1:
-                f()
-    need("v", "ss", last[0])
-    v_l = did("vs", V.tensor_copy(T.offb[:, 0:HOME], T.raw[:, :]))
-    for kk in range(2):
-        v_home = did("vs", V.tensor_copy(T.offb[:, HOME + N * kk:HOME + N * kk + N], T.raw[:, LC + kk:HOME:LW]))
-    quant(NCH - 1)
+    def link(k, u, h, o):
+        a, first = QUAD.index(k), "xy".index(h[0])
+        b, name = PAIR * a + CAP * first, u + str(o)
+        here = T["z%d" % o][:, SL + b:SL + b + CAP * len(h)]
+        t = T.tmp[:, N * CAP * o + b:N * CAP * o + b + CAP * len(h)]
+        if "mm" + name in known:
+            bank = product(u, k, h, o)
+            step("e" + name, ["mm" + name], copy(here, bank))
+            if "a" + name in known:
+                step("a" + name, [pick("g", k, x, o) for x in h] + ["mm" + name], lambda: V.tensor_tensor(here, bank, t, Alu.add))
+        win, last = upto(2 * a, o)
+        earlier = win.indirect(T.offs[:, a, LC * first:LC * (first + len(h))])
+        step("g" + name, ["ls", g_z] + last, copy(t, earlier))
+        if "l" + name in known:
+            step("l" + name, [pick("e", k, x, o) for x in h] + ["ls", g_z] + last, lambda: V.tensor_tensor(here, earlier, here, Alu.add))
 
-    loc = 0
-    arr = []
-    for c in range(NCH - 1):
-        dests = chunks[c]
-        need("g", "vs", v_q[c])
-        for kind in range(2):
-            tr, tot = [], 0
-            for i, d in enumerate(dests):
-                dst = T.cores[d]
-                eng = topo.engines(core, dst)
-                n = len(eng) // len(dests)
-                rid, pnc = topo.addr(dst, core)
-                a = at[c] + CAP * i
-                b = start[c] + CAP * (r % len(dests))
-                if kind == 0:
-                    src, out = T.q[:, a:a + CAP].bitcast(dt.uint8), T.lq[:, b:b + CAP].bitcast(dt.uint8)
-                else:
-                    src, out = T.qsc[:, a:a + CAP], T.lsc[:, b:b + CAP]
-                tr.append(RemoteDMATransfer(dst_ids=[DstId(rid=rid, pnc=pnc)], dma_engine_mask=sum(1 << e for e in eng[i * n:(i + 1) * n]),
-                                            remote_sem=T.sem["a%d" % c], src=src, dst=out))
-                tot += n
-            g.remote_dma_fused(tr, local_sem=T.sem.loc)
-            loc += tot
-        arr.append(2 * tot)
-
-    bank_free = [0] * 8
-    use = [0]
-    z_in = {}
-    chain = [v_l] * NB
-
-    def product(st, o):
-        c = sums[st]
-        place = sum(len(chunks[x]) for x in sums[:st])
-        width = start[c + 1] - start[c]
-        n = max(TILE, width)
-        need("t", "vs", v_w[0])
-        if c < NCH - 1:
-            src, ssc, first = T.lq, T.lsc, start[c + 1] - n
-            need("t", "a%d" % c, arr[c])
+    def product(k, chunk, h, o):
+        name, width = k + str(o), CAP * len(h)
+        n = plan["t"].index("mm" + name)
+        after = ["w%d" % o]
+        if n >= 8:
+            old = plan["t"][n - 8][2:]
+            after.append("a" + old if "a" + old in plan["v"] else "e" + old)
+        if k == "S":
+            src, ssc, end = T.q, T.qsc, QW
+            after.append("q%d" % CH.index(k))
         else:
-            src, ssc, first = T.q, T.qsc, QW - n
-            need("t", "vs", v_q[c])
-        bk = use[0] % 8
-        use[0] += 1
-        need("t", "ss", bank_free[bk])
-        p = did("ps", g.tensor.matmul_mx(T.ps[:, 512 * bk:512 * bk + n], T.wq[:, 128 * o:128 * o + 128], T.wsc[:, 128 * o:128 * o + 128],
-                                         src[:, first:first + n], ssc[:, first:first + n], True, True))
-        need("s", "ps", p)
-        b = SL + CAP * place
-        bank_free[bk] = did("ss", S.activation(T["z%d" % o][:, b:b + width], T.ps[:, 512 * bk + n - width:512 * bk + n], Copy))
-        for i in range(width // CAP):
-            z_in[place + i, o] = bank_free[bk]
+            i = lands.index((chunk.replace("O", "M"), h[-1]))
+            src, ssc, end = T.lq, T.lsc, CAP * (i + 1)
+            after += [(sem, arrive[sem]) for sem in ["a%d%s" % (CH.index(x), y) for x, y in lands[i - 1:i + 1]]]
+        wide = max(TILE, width)
+        step("mm" + name, after, lambda: g.tensor.matmul_mx(T.ps[:, 512 * (n % 8):512 * (n % 8) + wide], T.wq[:, 128 * o:128 * o + 128], T.wsc[:, 128 * o:128 * o + 128],
+                                                            src[:, end - wide:end], ssc[:, end - wide:end], True, True))
+        return T.ps[:, 512 * (n % 8) + wide - width:512 * (n % 8) + wide]
 
-    for st in range(NCH):
-        for o in range(NB):
-            product(st, o)
+    def bags(o):
+        x, y = T.half[:, BAGS * o:BAGS * (o + 1)], T.acc[:, BAGS * o:BAGS * (o + 1)]
+        (wx, lx), (wy, ly) = upto(N - 1, o), upto(N, o)
+        step("x%d" % o, lx + ["lx"], (cast if "x%d" % o in plan["v"] else copy)(x, wx.indirect(T.offh[:, 0, :])))
+        step("y%d" % o, ly + ["x%d" % o, "ly"], lambda: V.tensor_tensor(y, wy.indirect(T.offh[:, 1, :]), x, Alu.add))
 
-    need("v", "gs", g_z)
-    need("s", "gs", g_z)
-    for i, o in [(i, o) for i in range(1, TAIL[0][0]) for o in range(NB)] + TAIL:
-        b = SL + CAP * i
-        z = T["z%d" % o]
-        need("v", "vs", chain[o])
-        need("v", "ss", z_in[i, o])
-        chain[o] = did("vs", V.tensor_tensor(z[:, b:b + CAP], z[:, 0:b].indirect(T.offb[:, LW * i:LW * i + LC]), z[:, b:b + CAP], Alu.add))
+    for o in range(NB):
+        for k in QUAD:
+            for u, h in [(k, "xy"), (HALVES[k][0], "x"), (HALVES[k][1], "y")]:
+                link(k, u, h, o)
+        bags(o)
 
-    pieces = PIECES
-    for qn, o, a, b in pieces:
-        y = T.acc[:, BAGS * o + a:BAGS * o + b]
-        win = T["z%d" % o][:, 0:ZW].indirect(T.offb[:, HOME + a // 16:HOME + b // 16])
-        need(qn, "vs", max(chain[o], v_home))
-        if qn == "v":
-            need("y", "vs", did("vs", V.tensor_copy(y, win)))
-            q = g.sync
-        else:
-            k = did("ss", S.activation(y, win, Copy))
-            q = S if o == 1 else g.sync
-            need("s" if o == 1 else "y", "ss", k)
-        q.dma_start(T.y[:, BAGS * o + a:BAGS * o + b], y).then_inc(T.sem.st, 16)
+    place = {}
+    for qn in plan:
+        k = cnt[qn]
+        for name in plan[qn]:
+            k += len(steps[name][1])
+            place[name] = (sems[qn], k)
+    for qn in plan:
+        for name in plan[qn]:
+            after, calls = steps[name]
+            most = {}
+            for sem, val in [place.get(x, x) for x in after]:
+                most[sem] = max(most.get(sem, 0), val)
+            for sem in most:
+                need(qn, sem, most[sem])
+            for f in calls:
+                did(qn, f())
 
-    need("g", "loc", loc)
-    for sem in ("gs", "vs", "ss", "ps"):
-        need("g", sem, cnt[sem])
-    need("g", "st", 16 * len(pieces))
+    need("y", *g_pw)
+    need("y", *place["scat"])
+    for i in range(N):
+        g.sync.dma_start(T.prw[16 * (i % 2) + i // 2:128:32, 0:BAGS], T.inv[16 * i:16 * i + NP, 0:BAGS]).then_inc(T.sem.ldt, 16)
+
+    for kind, to in sends:
+        tr = []
+        for c, d, eng in to:
+            rid, pnc = topo.addr(T.cores[d], core)
+            a = HW + PAD if CH[c] == "M" else PAD + start[c] + CAP * (d % 2)
+            b = CAP * lands.index((CH[c], "xy"[(r ^ d) % 2]))
+            if kind == "c":
+                src, out = T.q[:, a:a + CAP].bitcast(dt.uint8), T.lq[:, b:b + CAP].bitcast(dt.uint8)
+            else:
+                src, out = T.qsc[:, a:a + CAP], T.lsc[:, b:b + CAP]
+            tr.append(RemoteDMATransfer(dst_ids=[DstId(rid=rid, pnc=pnc)], dma_engine_mask=sum(1 << e for e in eng),
+                                        remote_sem=T.sem["a%d%s" % (c, "xy"[(r ^ d) % 2])], src=src, dst=out))
+            need("g", *place["q%d" % c])
+        g.remote_dma_fused(tr, local_sem=T.sem.loc)
+
+    for o in range(NB):
+        need("y", *place["y%d" % o])
+        g.sync.dma_start(T.y[:, BAGS * o:BAGS * (o + 1)], T.acc[:, BAGS * o:BAGS * (o + 1)]).then_inc(T.sem.st, 16)
+
+    need("g", "loc", sum(arrive.values()))
+    for qn in cnt:
+        need("g", sems[qn], cnt[qn])
+    need("g", "st", 16 * NB)

from concourse.bass import DstId, RemoteDMATransfer
from concourse.mybir import dt, AluOpType, ActivationFunctionType, AxisListType

N, CAP, BAGS, NB, ITEMS = 8, 96, 256, 3, 512
TILE = 128
PAD = TILE - CAP
PAIR = 2 * CAP
NP = N // 2
LC = CAP // 16
ZERO = 16
WIN = ZERO + 4 * ITEMS
INV = 464
SL = 8
ZW = SL + N * CAP
HC = BAGS // 16 // NP
LW = LC + HC
PV = 32 * LW
HW = PAD + N * CAP
QW = HW + 2 * TILE
CH = "MABPS"
QUAD = "AOBP"
HALVES = {"A": "CD", "B": "EF", "O": "SM", "P": "XY"}
YQ = "it0 it1 b0 ex w"
XQ = "jt0 jt1 b1"
VP = "zx zh i1 i2 o0 pos o1 o2 o3 bo boff"
VQ = "p00 p01 p02 p03 scat q0 p10 p11 p12 p13 p20 q1 p21 p22 p23 p30 q2 p31 p32 p33 turn q3 red w2 w0 w1 p40 p41 p42 p43 ls q4 lx ly"
SQ = "i3 home vals f00 f01 f02 f03 f10 f11 F12 F20 F22 F30 F32 rows f40 twice f41 f42 f43 collect spread"
VS = "lM2 lM0 lM1 aS2 aS0 aS1 lB0 lB1 lX0 aB2 lX1 aY0 lX2 aY1 lY2 y0 y1 y2"
SS = "eA2 eM2 eA0 eM0 eA1 eM1 gS2 gS0 gS1 eB0 eB1 gB2 eX0 eX1 gY0 eX2 gY1 eY2 x0 x1 x2"
GQ = "c0 s0 c1 s1 c2 s2 c3x s3 c3y"
TQ = "A2 M2 A0 M0 A1 M1 B0 S2 S0 B1 S1 X0 X1 X2 B2 Y2 Y0 Y1"
F32, BF, I32, U16 = "float32", "bfloat16", "int32", "uint16"
SCRATCH = {
    "exw": ("sbuf", [128, WIN], BF),
    "wt": ("sbuf", [128, 512 * NB], BF),
    "wq": ("sbuf", [128, 128 * NB], "float8_e4m3fn_x4"),
    "wsc": ("sbuf", [128, 128 * NB], "uint8"),
    "lraw": ("sbuf", [128, N, 2 * LC], I32),
    "off": ("sbuf", [128, N, 8 * LC], U16),
    "hu": ("sbuf", [128, 4 * N * CAP], BF),
    "h": ("sbuf", [128, 4 * HW], BF),
    "q": ("sbuf", [128, QW], "float8_e4m3fn_x4"),
    "qsc": ("sbuf", [128, QW], "uint8"),
    "lq": ("sbuf", [128, (N - 1) * CAP], "float8_e4m3fn_x4"),
    "lsc": ("sbuf", [128, (N - 1) * CAP], "uint8"),
    "bagg": ("sbuf", [128, (N - 1) * LC], I32),
    "pos": ("sbuf", [128, LC], I32),
    "dumpo": ("sbuf", [128, LC], I32),
    "bo": ("sbuf", [128, LW], F32),
    "ib": ("sbuf", [128, HC], F32),
    "boff": ("sbuf", [128, LW], U16),
    "ip": ("sbuf", [128, 1], I32),
    "ipi": ("sbuf", [128, 3], I32),
    "ipf": ("sbuf", [128, 6], F32),
    "io1": ("sbuf", [128, CAP], F32),
    "vals": ("sbuf", [128, CAP], F32),
    "inv": ("sbuf", [128, INV], F32),
    "prw": ("sbuf", [128, INV], F32),
    "once": ("sbuf", [128, 16 * LW], F32),
    "pv": ("sbuf", [128, LW, 32], F32),
    "pvt": ("sbuf", [128, 2 * LW, 16], F32),
    "raw": ("sbuf", [128, NP, 2 * LW], F32),
    "offs": ("sbuf", [128, NP, 2 * LC], U16),
    "offh": ("sbuf", [128, 2, NP * HC], U16),
    "tmp": ("sbuf", [128, NB * NP * PAIR], F32),
    "half": ("sbuf", [128, NB * BAGS], F32),
    "acc": ("sbuf", [128, NB * BAGS], F32),
    "ps": ("psum", [128, 4096], F32),
}
for _k in range(NB):
    SCRATCH["z%d" % _k] = ("sbuf", [128, ZW], F32)
SEMAPHORES = ["ldl", "ldx", "ldb", "ldw", "ldt", "vs", "ss", "ps", "gs", "loc", "st"] + ["a%d%s" % (_c, _h) for _c in range(5) for _h in "xy"]


def rank_program(g, core, T, topo):
    r = T.rank_of(core)
    if r is None:
        return
    Alu, Copy, Same = AluOpType, ActivationFunctionType.Copy, ActivationFunctionType.Identity
    V, S = g.vector, g.scalar
    order = sorted(range(1, NP), key=lambda x: (topo.host(T.cores[2 * x]) == topo.host(T.cores[0]), -x))
    who = {k: [2 * (r // 2 ^ x) + m for m in range(2)] for k, x in zip("ABP", order)}
    who.update(M=[r ^ 1], S=[r])
    chunks = [who[k] for k in CH]
    NCH = len(chunks)
    start = [CAP * sum(len(c) for c in chunks[:i]) for i in range(NCH + 1)]
    pairs = [[r, r ^ 1] if k == "O" else who[k] for k in QUAD]
    lands = [(k.replace("O", "M"), h) for k in QUAD for h in "xy" if k + h != "Ox"]
    plan = {"v": " ".join([VP, VQ, VS]).split(), "s": (SQ + " " + SS).split(), "t": ["mm" + x for x in TQ.split()]}

    seen = {}
    queues = {"v": V, "s": S, "t": g.tensor, "y": g.sync, "g": g}
    sems = {"v": "vs", "s": "ss", "t": "ps", "g": "gs"}
    cnt = {"v": 0, "s": 0, "t": 0, "g": 0}

    def need(qn, sem, val):
        if val > seen.get((qn, sem), 0):
            queues[qn].wait_ge(T.sem[sem], val)
            seen[(qn, sem)] = val

    def did(qn, ins):
        ins.then_inc(T.sem[sems[qn]], 1)
        cnt[qn] += 1
        return cnt[qn]

    loads = {"ex": (T.exw[:, ZERO:WIN], T.ex[:, :], "ldx"), "w": (T.wt[:, :], T.w[:, :], "ldw")}
    for i in range(2):
        first = LC * ((r + i) % 2)
        loads["b%d" % i] = (T.bagg[16 * i:16 * i + 16, :], T.bag[:, first:first + (N - 1) * LC], "ldb")
        loads["it%d" % i] = (T.lraw[16 * i:16 * i + 16, 0:NP, :], T["it"][:, :], "ldl")
        loads["jt%d" % i] = (T.lraw[16 * i:16 * i + 16, NP:N, :], T["it2"][:, :], "ldl")
    for q, names in ((g.sync, YQ), (S, XQ)):
        for name in names.split():
            out, in_, sem = loads[name]
            q.dma_start(out, in_).then_inc(T.sem[sem], 16)

    def ramp(ap, pattern, base=0):
        return ("gs", did("g", g.iota(ap, pattern, base, 0, allow_small_or_imprecise_dtypes=True)))
    g_ip = ("gs", did("g", g.iota(T.ip[:, :], [[1, 1]], 0, 1)))
    ramp(T.ib[:, :], [[16, HC]])
    g_io = ramp(T.io1[:, :], [[1, CAP]], SL)
    g_du = ("gs", did("g", g.iota(T.dumpo[:, :], [[16, LC]], BAGS, 1)))
    g_inv = ramp(T.inv[:, :], [[0, INV]])
    g_pw = ramp(T.prw[:, :], [[0, INV]])
    for o in range(NB):
        g_z = ramp(T["z%d" % o][:, 0:SL], [[0, SL]])

    steps = {}

    def step(name, after, *calls):
        steps[name] = (after, calls)

    def copy(out, in_):
        return lambda: S.activation(out, in_, Copy)

    def scal(out, in_, *ops):
        return lambda: V.tensor_scalar(out, in_, *ops)

    def cast(out, in_):
        return lambda: V.tensor_copy(out, in_)

    step("zx", [], lambda: V.memset(T.exw[:, 0:ZERO], 0.0))
    step("zh", [], lambda: V.memset(T.h[:, 0:4 * PAD], 0.0))
    step("i1", [g_ip], scal(T.ipi[:, 0:1], T.ip[:, :], 4, None, Alu.arith_shift_right), scal(T.ipi[:, 1:2], T.ip[:, :], 5, None, Alu.arith_shift_right),
         scal(T.ipi[:, 2:3], T.ip[:, :], 15, None, Alu.bitwise_and))
    step("i2", ["i1"], cast(T.ipf[:, 0:3], T.ipi[:, :]))
    grp, quad, row, bag0, before, slot0 = [T.ipf[:, k:k + 1] for k in range(6)]
    step("i3", ["i2"], lambda: S.activation(slot0, grp, Copy, scale=float(CAP)), lambda: S.activation(bag0, quad, Same, bias=row, scale=16.0 * HC),
         lambda: S.activation(before, row, ActivationFunctionType.Sign, bias=quad, scale=-1.0))
    step("vals", ["i3", g_io], lambda: S.activation(T.vals[:, :], T.io1[:, :], Same, bias=slot0))
    step("home", ["i3", g_io], lambda: S.activation(T.bo[:, LC:LW], T.ib[:, :], Same, bias=bag0))
    step("o0", [("ldl", 64)], *[scal(T.off[32 * a:32 * a + 32, :, 0:2 * LC], T.lraw[0:32, :, :], 4.0, float(ZERO), Alu.mult, Alu.add) for a in range(4)])
    for t in range(1, 4):
        step("o%d" % t, ["o0"], scal(T.off[:, :, 2 * LC * t:2 * LC * (t + 1)], T.off[:, :, 0:2 * LC], float(t), None, Alu.add))
    step("pos", [("ldb", 32)], *[scal(T.pos[32 * a:32 * a + 32, :], T.bagg[0:32, LC * min(p):LC * min(p) + LC], 2 * BAGS - 1, None, Alu.bitwise_and)
                                 for a, p in enumerate(pairs)])
    step("bo", ["pos", g_du], lambda: V.tensor_tensor(T.bo[:, 0:LC], T.pos[:, :], T.dumpo[:, :], Alu.min))
    step("boff", ["bo", "home"], cast(T.boff[:, :], T.bo[:, :]))
    step("scat", ["boff", "vals", g_inv], cast(T.inv[:, 0:INV].indirect(T.boff[:, 0:LC]), T.vals[:, :]))

    def items(c, t, second, n=1):
        d = chunks[c][0]
        l = 2 * LC * t + LC * (d % 2)
        return T.exw[:, 0:WIN].indirect(T.off[:, second * NP + d // 2, l:l + n * LC * len(chunks[c])])

    def parts(c, t):
        w = start[c + 1] - start[c]
        u = T.hu[:, 4 * start[c] + t * w:4 * start[c] + (t + 1) * w]
        one, two = "f%d%d" % (c, t), "F%d%d" % (c, t - t % 2)
        step(one, [("ldx", 16), "zx", "o%d" % t], (cast if one in plan["v"] else copy)(u, items(c, t, 0)))
        if t % 2 == 0 and two in plan["s"]:
            step(two, [("ldx", 16), "zx", "o%d" % (t + 1)], copy(T.hu[:, 4 * start[c] + t * w:4 * start[c] + (t + 2) * w], items(c, t, 0, 2)))
        step("p%d%d" % (c, t), [two if two in plan["s"] else one, "o%d" % t],
             lambda: V.tensor_tensor(T.h[:, 4 * (PAD + start[c]) + t:4 * (PAD + start[c + 1]):4], items(c, t, 1), u, Alu.add))

    def quant(c):
        b = PAD + start[c + 1]
        a = min(PAD + start[c], b - TILE)
        o = HW + TILE * "MS".index(CH[c]) if CH[c] in "MS" else a
        step("q%d" % c, ["p%d%d" % (x, t) for t in range(4) for x in range(max(0, c - (a < PAD + start[c])), c + 1)] + ["zh"] * (a < PAD), lambda: V.quantize_mx(T.q[:, o:o + b - a], T.qsc[:, o:o + b - a], T.h[:, 4 * a:4 * b]))

    def weights(o):
        step("w%d" % o, [("ldw", 16)], lambda: V.quantize_mx(T.wq[:, 128 * o:128 * o + 128], T.wsc[:, 128 * o:128 * o + 128], T.wt[:, 512 * o:512 * o + 512]))

    for c in range(NCH):
        quant(c)
        for t in range(4):
            parts(c, t)
    for o in range(NB):
        weights(o)

    step("rows", [("ldt", 16 * N), "boff", "i3"],
         lambda: S.activation(T.once[:, 0:CAP], T.prw[:, 0:INV].indirect(T.boff[:, 0:LC]), Same, scale=before),
         copy(T.once[:, CAP:16 * LW], T.prw[:, 0:INV].indirect(T.boff[:, LC:LW])))
    step("twice", ["rows"], *[copy(T.pv[:, :, 16 * d:16 * d + 16], T.once[:, :]) for d in range(2)])
    step("turn", ["twice"], lambda: V.transpose(T.pvt[:, :, :], T.pv[:, :, :]))
    step("red", ["turn"], lambda: V.tensor_reduce(T.raw[:, 0, :], T.pvt[:, :, 0:NP], AxisListType.X, Alu.max))
    step("collect", ["red"], *[copy(T.raw[0:32, a, :], T.raw[32 * a:32 * a + 32, 0, :]) for a in range(1, NP)])
    step("spread", ["collect"], *[copy(T.raw[32 * a:32 * a + 32, :, :], T.raw[0:32, :, :]) for a in range(1, NP)])
    step("ls", ["spread"], *[cast(T.offs[:, :, LC * h:LC * (h + 1)], T.raw[:, :, h:2 * LC:2]) for h in range(2)])
    step("lx", ["spread"], cast(T.offh[:, 0, :], T.raw[:, :, 2 * LC:2 * LW:2]))
    step("ly", ["spread"], cast(T.offh[:, 1, :], T.raw[:, :, 2 * LC + 1:2 * LW:2]))

    sends, arrive = [], {}
    for x in GQ.split():
        to = [(int(y[0]), d) for y in x[1:].split("+") for d in chunks[int(y[0])] if y[1:] in ("", "xy"[(r ^ d) % 2])]
        to.sort(key=lambda cd: (cd[0], (r ^ cd[1]) % 2))
        eng = topo.engines(core, T.cores[to[0][1]])
        n = [len(eng) // (1 << (len(to) - 1).bit_length())] * len(to)
        n[0] += len(eng) - sum(n)
        sends.append((x[0], [(c, d, eng[sum(n[:i]):sum(n[:i + 1])]) for i, (c, d) in enumerate(to)]))
        for i, (c, d) in enumerate(to):
            sem = "a%d%s" % (c, "xy"[(r ^ d) % 2])
            arrive[sem] = arrive.get(sem, 0) + n[i]

    known = plan["v"] + plan["s"] + plan["t"]

    def pick(kinds, k, h, o):
        return [x + u + str(o) for x in kinds for u in (k, HALVES[k]["xy".index(h)]) if x + u + str(o) in known][0]

    def upto(n, o):
        return T["z%d" % o][:, 0:SL + CAP * n], [pick("lae", QUAD[i // 2], "xy"[i % 2], o) for i in range(n)]

    def link(k, u, h, o):
        a, first = QUAD.index(k), "xy".index(h[0])
        b, name = PAIR * a + CAP * first, u + str(o)
        here = T["z%d" % o][:, SL + b:SL + b + CAP * len(h)]
        t = T.tmp[:, N * CAP * o + b:N * CAP * o + b + CAP * len(h)]
        if "mm" + name in known:
            bank = product(u, k, h, o)
            step("e" + name, ["mm" + name], copy(here, bank))
            if "a" + name in known:
                step("a" + name, [pick("g", k, x, o) for x in h] + ["mm" + name], lambda: V.tensor_tensor(here, bank, t, Alu.add))
        win, last = upto(2 * a, o)
        earlier = win.indirect(T.offs[:, a, LC * first:LC * (first + len(h))])
        step("g" + name, ["ls", g_z] + last, copy(t, earlier))
        if "l" + name in known:
            step("l" + name, [pick("e", k, x, o) for x in h] + ["ls", g_z] + last, lambda: V.tensor_tensor(here, earlier, here, Alu.add))

    def product(k, chunk, h, o):
        name, width = k + str(o), CAP * len(h)
        n = plan["t"].index("mm" + name)
        after = ["w%d" % o]
        if n >= 8:
            old = plan["t"][n - 8][2:]
            after.append("a" + old if "a" + old in plan["v"] else "e" + old)
        if k == "S":
            src, ssc, end = T.q, T.qsc, QW
            after.append("q%d" % CH.index(k))
        else:
            i = lands.index((chunk.replace("O", "M"), h[-1]))
            src, ssc, end = T.lq, T.lsc, CAP * (i + 1)
            after += [(sem, arrive[sem]) for sem in ["a%d%s" % (CH.index(x), y) for x, y in lands[i - 1:i + 1]]]
        wide = max(TILE, width)
        step("mm" + name, after, lambda: g.tensor.matmul_mx(T.ps[:, 512 * (n % 8):512 * (n % 8) + wide], T.wq[:, 128 * o:128 * o + 128], T.wsc[:, 128 * o:128 * o + 128],
                                                            src[:, end - wide:end], ssc[:, end - wide:end], True, True))
        return T.ps[:, 512 * (n % 8) + wide - width:512 * (n % 8) + wide]

    def bags(o):
        x, y = T.half[:, BAGS * o:BAGS * (o + 1)], T.acc[:, BAGS * o:BAGS * (o + 1)]
        (wx, lx), (wy, ly) = upto(N - 1, o), upto(N, o)
        step("x%d" % o, lx + ["lx"], (cast if "x%d" % o in plan["v"] else copy)(x, wx.indirect(T.offh[:, 0, :])))
        step("y%d" % o, ly + ["x%d" % o, "ly"], lambda: V.tensor_tensor(y, wy.indirect(T.offh[:, 1, :]), x, Alu.add))

    for o in range(NB):
        for k in QUAD:
            for u, h in [(k, "xy"), (HALVES[k][0], "x"), (HALVES[k][1], "y")]:
                link(k, u, h, o)
        bags(o)

    place = {}
    for qn in plan:
        k = cnt[qn]
        for name in plan[qn]:
            k += len(steps[name][1])
            place[name] = (sems[qn], k)
    for qn in plan:
        for name in plan[qn]:
            after, calls = steps[name]
            most = {}
            for sem, val in [place.get(x, x) for x in after]:
                most[sem] = max(most.get(sem, 0), val)
            for sem in most:
                need(qn, sem, most[sem])
            for f in calls:
                did(qn, f())

    need("y", *g_pw)
    need("y", *place["scat"])
    for i in range(N):
        g.sync.dma_start(T.prw[16 * (i % 2) + i // 2:128:32, 0:BAGS], T.inv[16 * i:16 * i + NP, 0:BAGS]).then_inc(T.sem.ldt, 16)

    for kind, to in sends:
        tr = []
        for c, d, eng in to:
            rid, pnc = topo.addr(T.cores[d], core)
            a = HW + PAD if CH[c] == "M" else PAD + start[c] + CAP * (d % 2)
            b = CAP * lands.index((CH[c], "xy"[(r ^ d) % 2]))
            if kind == "c":
                src, out = T.q[:, a:a + CAP].bitcast(dt.uint8), T.lq[:, b:b + CAP].bitcast(dt.uint8)
            else:
                src, out = T.qsc[:, a:a + CAP], T.lsc[:, b:b + CAP]
            tr.append(RemoteDMATransfer(dst_ids=[DstId(rid=rid, pnc=pnc)], dma_engine_mask=sum(1 << e for e in eng),
                                        remote_sem=T.sem["a%d%s" % (c, "xy"[(r ^ d) % 2])], src=src, dst=out))
            need("g", *place["q%d" % c])
        g.remote_dma_fused(tr, local_sem=T.sem.loc)

    for o in range(NB):
        need("y", *place["y%d" % o])
        g.sync.dma_start(T.y[:, BAGS * o:BAGS * (o + 1)], T.acc[:, BAGS * o:BAGS * (o + 1)]).then_inc(T.sem.st, 16)

    need("g", "loc", sum(arrive.values()))
    for qn in cnt:
        need("g", sems[qn], cnt[qn])
    need("g", "st", 16 * NB)
